import numpy as np
import ml_dtypes


def mxq(x, axis, fmt="e4m3"):
    dtype, down = {"e4m3": (ml_dtypes.float8_e4m3fn, 7), "e5m2": (ml_dtypes.float8_e5m2, 14)}[fmt]
    v = np.moveaxis(np.asarray(x, np.float32).astype(ml_dtypes.bfloat16).astype(np.float64), axis, -1)
    blocks = v.reshape(v.shape[:-1] + (-1, 32))
    amax = np.abs(blocks).max(-1, keepdims=True)
    byte = np.maximum(np.where(amax > 0, np.frexp(amax)[1] - 1 + 127, 0) - down, 1)
    scale = np.exp2(byte - 127.0)
    codes = (blocks / scale).astype(np.float32).astype(dtype).astype(np.float64)
    return np.moveaxis((codes * scale).reshape(v.shape), -1, axis)


WIDE = False


def mx_kscale(k):
    if not WIDE:
        return np.ones(k)
    levels = np.array([10, -10, 5, -5, 0])
    if k % 512:
        return np.exp2(np.random.permutation(np.resize(levels, k // 32))).repeat(32)
    a = np.empty((k // 512, 16))
    for p in range(k // 512):
        a[p, :8] = np.random.permutation(np.resize(levels, 8))
        for g in range(8):
            far = levels[np.abs(levels - a[p, g]) >= 10]
            a[p, g + 8] = far[np.random.randint(len(far))]
    return np.exp2(a.ravel()).repeat(32)


def f64(x):
    return np.asarray(x).astype(np.float64)


def striped(idx):
    return np.tile(idx.reshape(-1, 16).T, (8, 1)).astype(np.uint16)


def unstriped(offs):
    return offs[:16].T.reshape(-1).astype(np.int64)


E2M1 = np.array([0.0, 0.5, 1.0, 1.5, 2.0, 3.0, 4.0, 6.0, -0.0, -0.5, -1.0, -1.5, -2.0, -3.0, -4.0, -6.0])


def pack_weight(w, fmt):
    k, n = w.shape
    w = f64(np.asarray(w, np.float32).astype(ml_dtypes.bfloat16)).reshape(k // 32, 32, n)
    amax = np.abs(w).max(1)
    if fmt == "e4m3":
        byte = np.frexp(amax)[1] - 1 + 127 - 7
    else:
        mant, ex = np.frexp(amax / 6.0)
        byte = np.where(mant > 0.5, ex, ex - 1) + 127
    byte = np.clip(np.where(amax > 0, byte, 1), 1, 254)
    scaled = (w * np.exp2(127.0 - byte)[:, None, :]).reshape(k, n).astype(np.float32)
    by_word = np.ascontiguousarray(scaled.reshape(k // 512, 128, 4, n).transpose(0, 1, 3, 2))
    if fmt == "e4m3":
        words = by_word.astype(ml_dtypes.float8_e4m3fn).view(np.uint8)
    else:
        c = by_word.astype(ml_dtypes.float4_e2m1fn).view(np.uint8) & 0xF
        words = (c[..., 0::2] | (c[..., 1::2] << 4)).reshape(k // 512, 128, 2 * n)
    return np.ascontiguousarray(words), np.ascontiguousarray(byte.astype(np.uint8).reshape(k // 512, 16, n))


def unpack_weight(words, scales, fmt):
    g, _, n = scales.shape
    words = np.ascontiguousarray(words).reshape(g, 128, n, -1)
    if fmt == "e4m3":
        vals = words.view(ml_dtypes.float8_e4m3fn).astype(np.float64)
    else:
        nib = np.empty((g, 128, n, 4), np.uint8)
        nib[..., 0::2] = words & 0xF
        nib[..., 1::2] = words >> 4
        vals = E2M1[nib]
    vals = vals * np.repeat(np.exp2(scales.astype(np.float64) - 127.0), 8, axis=1)[..., None]
    return vals.transpose(0, 1, 3, 2).reshape(g * 512, n)


def gelu(v):
    return 0.5 * v * (1.0 + np.tanh(np.sqrt(2.0 / np.pi) * (v + 0.044715 * v**3)))


def bf(x):
    return np.asarray(x, np.float32).astype(ml_dtypes.bfloat16)


def planes(Y):
    n, m = Y.shape
    b = f64(bf(Y)).reshape(n // 32, 32, m)
    amax = np.abs(b).max(1)
    byte = np.clip(np.where(amax > 0, np.frexp(amax)[1] - 1 + 127 - 7, 1), 1, 254)
    codes = (b * np.exp2(127.0 - byte)[:, None, :]).reshape(n, m).astype(np.float32).astype(ml_dtypes.float8_e4m3fn).view(np.uint8)
    words = codes.reshape(n // 512, 128, 4, m).transpose(0, 1, 3, 2)
    return np.ascontiguousarray(words), np.ascontiguousarray(byte.astype(np.uint8).reshape(n // 512, 16, m))


K, T, S, T2, H, M, N = 1024, 2048, 512, 1024, 512, 1024, 512

def setup_inputs():
    n = np.random.standard_normal
    s, u, um = mx_kscale(K)[:, None], mx_kscale(H)[:, None], mx_kscale(M)[:, None]
    amp = np.exp(0.8 * n(N))
    tab_words, tab_scales = pack_weight(n((K, T)) * s, "e4m3")
    tab2_words, tab2_scales = pack_weight(n((K, T)) * s, "e4m3")
    w2_words, w2_scales = pack_weight(n((K, H)) * 0.54 / np.sqrt(K) / s, "e2m1")
    wo_words, wo_scales = pack_weight(n((M, N)) * 0.9 / np.sqrt(M) / um * amp, "e4m3")
    return {"tab_words": tab_words, "tab_scales": tab_scales, "tab2_words": tab2_words, "tab2_scales": tab2_scales,
            "offs": striped(np.random.permutation(T)[:S]), "offs2": striped(np.random.permutation(T)[:S]),
            "offs3": striped(np.random.permutation(T2)[:S]), "offs4": striped(np.random.permutation(T2)[:S]),
            "w1": (n((K, H)) * 1.3 / np.sqrt(K) / s).astype(np.float32),
            "w2_words": w2_words, "w2_scales": w2_scales,
            "wg1": np.exp(0.3 * n((128, S))).astype(np.float32), "wg2": np.exp(0.3 * n((128, S))).astype(np.float32),
            "tpl": (0.4 * n((H, T2))).astype(np.float32),
            "gz": (np.random.uniform(0.6, 1.5, H) * u[:, 0]).astype(np.float32),
            "wq": (n((H, M)) * 1.7 / np.sqrt(H) / u).astype(np.float32),
            "gf": (np.random.uniform(0.6, 1.5, M) * um[:, 0]).astype(np.float32),
            "wo_words": wo_words, "wo_scales": wo_scales,
            "wd": (n((H, N)) * 0.9 / np.sqrt(H) / u * amp).astype(np.float32)}

def reference(tab_words, tab_scales, tab2_words, tab2_scales, offs, offs2, offs3, offs4, w1, w2_words, w2_scales,
              wg1, wg2, tpl, gz, wq, gf, wo_words, wo_scales, wd):
    v = unpack_weight(tab_words, tab_scales, "e4m3")[:, unstriped(offs)]
    v2 = unpack_weight(tab2_words, tab2_scales, "e4m3")[:, unstriped(offs2)]
    h1 = np.tanh(mxq(f64(w1), 0, "e4m3").T @ v)
    h2 = np.sin(unpack_weight(w2_words, w2_scales, "e2m1").T @ v2)
    pa = np.zeros((H, T2))
    pa[:, unstriped(offs3)] = np.tile(f64(wg1), (H // 128, 1)) * h1
    pb = np.zeros((H, T2))
    pb[:, unstriped(offs4)] = np.tile(f64(wg2), (H // 128, 1)) * h2
    z = (f64(tpl) + pa + pb) * f64(gz)[:, None]
    zq = mxq(z, 0, "e4m3")
    f = np.tanh(mxq(f64(wq), 0, "e4m3").T @ zq) * f64(gf)[:, None]
    wo = unpack_weight(wo_words, wo_scales, "e4m3")
    y = wo.T @ mxq(f, 0, "e4m3") + mxq(f64(wd), 0, "e4m3").T @ zq
    words, scales = planes(y)
    return y, words, scales

@@ -1,0 +1,421 @@
+import math
+from contextlib import ExitStack
+
+import concourse.mybir as mybir
+from concourse.masks import make_identity
+
+K, T, S, T2, H, M, N = 1024, 2048, 512, 1024, 512, 1024, 512
+FLOPS = 2 * (2 * K * H * S + H * M * T2 + M * N * T2 + H * N * T2)
+
+F32 = mybir.dt.float32
+BF16 = mybir.dt.bfloat16
+I32 = mybir.dt.int32
+U32 = mybir.dt.uint32
+U16 = mybir.dt.uint16
+U8 = mybir.dt.uint8
+FP8X4 = mybir.dt.float8_e4m3fn_x4
+FP4X4 = mybir.dt.float4_e2m1fn_x4
+ALU = mybir.AluOpType
+ACT = mybir.ActivationFunctionType
+
+P = 128
+PACK = 4
+QUADS = 4
+SLOTS = H // P
+LAST = SLOTS - 1
+CHUNK = 128
+CHUNKS = T2 // CHUNK
+BANK_CHUNKS = 4
+Z_GROUPS = (1,1,2,2,2,)
+Y_ON_SCALAR = (1,3,5,6,7,)
+SUM_BANKS = (4, 6, 4, 2)
+ROUND = 1.5 * 2.0**23
+
+
+def tile_list_spaxel_sky_kinematics_kernel(
+    tc, tab_words, tab_scales, tab2_words, tab2_scales, offs, offs2, offs3, offs4, w1, w2_words, w2_scales,
+    wg1, wg2, tpl, gz, wq, gf, wo_words, wo_scales, wd, out_0, out_1, out_2,
+):
+    nc = tc.nc
+    with ExitStack() as ctx:
+        lists = ctx.enter_context(tc.tile_pool(name="lists", bufs=1))
+        keep = ctx.enter_context(tc.tile_pool(name="keep", bufs=1))
+        ring = ctx.enter_context(tc.tile_pool(name="ring", bufs=2))
+        psum = ctx.enter_context(tc.psum_pool(name="psum", bufs=1))
+
+        def held(shape, dtype, name, tag=None):
+            return keep.tile(shape, dtype, name=name, tag=tag or name, align_bytes=64)
+
+        def staged(shape, dtype, name, bufs):
+            return ring.tile(shape, dtype, name=name, tag=name, bufs=bufs, align_bytes=64)
+
+        def bank(number, shape):
+            return psum.tile(shape, F32, name="bank%d" % number, tag="bank%d" % number)
+
+        def load_list(source, name):
+            tile = lists.tile([P, S // 16], U16, name=name)
+            nc.sync.dma_start(tile[:], source)
+            return tile
+
+        def load_words(words, a, name):
+            tile = held([P, T], U32, name)
+            nc.sync.dma_start(tile[:].bitcast(I32), words[a].rearrange("p t i -> p (t i)").bitcast(I32))
+            return tile
+
+        def load_scales_side_by_side(queue, tile, scales):
+            for q in range(QUADS):
+                queue.dma_start(
+                    tile[32 * q : 32 * q + 4, :].bitcast(I32).rearrange("r (a w) -> r a w", a=2),
+                    scales[:, 4 * q : 4 * q + 4, :].rearrange("a r c -> r a c").bitcast(I32),
+                )
+
+        def load_scales_stacked(queue, tile, scales):
+            for q in range(QUADS):
+                queue.dma_start(
+                    tile[32 * q : 32 * q + 8, :].bitcast(I32), scales[:, 4 * q : 4 * q + 4, :].bitcast(I32)
+                )
+
+        def load_rows(rows, name, tag):
+            tile = held([P, PACK, rows.shape[1]], F32, name, tag)
+            nc.sync.dma_start(tile[:], rows.rearrange("(p i) c -> p i c", i=PACK))
+            return tile
+
+        def gather(window, offsets, dtype, name):
+            picked = held([P, S], dtype, name)
+            nc.vector.tensor_copy(picked[:], window.indirect(offsets[:]))
+            return picked
+
+        def quantize(rounded, name, bufs=None):
+            width = rounded.shape[1] // PACK
+            if bufs is None:
+                codes = held([P, width], U32, name + "_codes")
+                scales = held([P, width], U8, name + "_scales")
+            else:
+                codes = staged([P, width], U32, name + "_codes", bufs)
+                scales = staged([P, width], U8, name + "_scales", bufs)
+            nc.vector.quantize_mx(out=codes[:].bitcast(FP8X4), scales=scales[:], in_=rounded)
+            return codes, scales
+
+        def round_plain(raw):
+            rounded = staged([P, PACK * 512], BF16, "rounded", 3)
+            for half in range(2):
+                nc.scalar.copy(
+                    rounded[:, 1024 * half : 1024 * (half + 1)].rearrange("p (c n i) -> p c i n", n=4, i=PACK),
+                    raw[:, :, 256 * half : 256 * (half + 1)].rearrange("p i (c n) -> p c i n", n=4),
+                )
+            return rounded
+
+        def round_dealt(raw):
+            rounded = staged([P, PACK * 512], BF16, "rounded", 3)
+            dealt = rounded[:].rearrange("p (t q i) -> p q i t", t=PACK, i=PACK)
+            source = raw[:].rearrange("p i (q t) -> p q i t", t=PACK)
+            for half in range(2):
+                nc.scalar.copy(dealt[:, 64 * half : 64 * (half + 1)], source[:, 64 * half : 64 * (half + 1)])
+            return rounded
+
+        sky_scales_raw = held([P, 2 * T], U8, "sky_scales_raw")
+        nc.vector.memset(sky_scales_raw[:].bitcast(I32), 0)
+        w2_scale_planes = held([P, 2 * H], U8, "w2_scale_planes")
+        nc.gpsimd.memset(w2_scale_planes[:].bitcast(I32), 0)
+        spax_scales_raw = held([P, T], U8, "spax_scales_raw")
+        nc.gpsimd.memset(spax_scales_raw[:].bitcast(I32), 0)
+        wo_scales_raw = held([P, N], U8, "wo_scales_raw")
+        nc.gpsimd.memset(wo_scales_raw[:].bitcast(I32), 0)
+
+        sky_list = load_list(offs2, "sky_list")
+        sky_places = load_list(offs4, "sky_places")
+        spax_list = load_list(offs, "spax_list")
+        spax_places = load_list(offs3, "spax_places")
+        gz_cols = held([P, SLOTS], F32, "gz_cols")
+        with nc.allow_non_contiguous_dma(reason="one gain a partition and slot"):
+            nc.sync.dma_start(gz_cols[:], gz.rearrange("(s p) -> p s", p=P))
+        gf_cols = held([P, 2, PACK], F32, "gf_cols")
+        nc.sync.dma_start(gf_cols[:], gf.rearrange("(a p t) -> p a t", a=2, t=PACK))
+        sky_words = [load_words(tab2_words, 0, "sky_words0")]
+        w2_codes = held([P, 2, 2 * H], U8, "w2_codes")
+        nc.sync.dma_start(w2_codes[:].bitcast(I32), w2_words.rearrange("a p c -> p a c").bitcast(I32))
+        load_scales_side_by_side(nc.sync, sky_scales_raw, tab2_scales)
+        sky_words.append(load_words(tab2_words, 1, "sky_words1"))
+        load_scales_side_by_side(nc.sync, w2_scale_planes, w2_scales)
+        spax_words = [load_words(tab_words, 0, "spax_words0")]
+        wg2_rows = held([P, S], F32, "wg2_rows")
+        nc.sync.dma_start(wg2_rows[:], wg2)
+        load_scales_stacked(nc.sync, spax_scales_raw, tab_scales)
+        spax_words.append(load_words(tab_words, 1, "spax_words1"))
+        w1_raw = [load_rows(w1[512 * a : 512 * (a + 1), :], "w1_raw%d" % a, "w1_raw%d" % a) for a in range(2)]
+        wg1_rows = held([P, S], F32, "wg1_rows")
+        nc.sync.dma_start(wg1_rows[:], wg1)
+
+        identity = held([P, P], F32, "identity")
+        make_identity(nc, identity[:])
+
+        sky_codes = [gather(sky_words[0][:], sky_list, U32, "sky_codes0")]
+        sky_scales = [
+            gather(sky_scales_raw[:, a * T : (a + 1) * T], sky_list, U8, "sky_scales%d" % a) for a in range(2)
+        ]
+        sky_codes.append(gather(sky_words[1][:], sky_list, U32, "sky_codes1"))
+
+        wq_raw = [load_rows(wq[:, 512 * a : 512 * (a + 1)], "wq_raw%d" % a, "sky_words%d" % a) for a in range(2)]
+        tpl_rows = []
+        for s in range(SLOTS):
+            rows = held([P, T2], F32, "tpl_rows%d" % s)
+            nc.sync.dma_start(rows[:], tpl[P * s : P * (s + 1), :])
+            tpl_rows.append(rows)
+
+        sky_pages = [held([P, T2], F32, "sky_page%d" % n) for n in range(2)]
+        spax_pages = [held([P, T2], F32, "spax_page%d" % n) for n in range(2)]
+        for page in sky_pages + spax_pages:
+            nc.vector.memset(page[:], 0.0)
+
+        gz_spread = bank(0, [P, P])
+        nc.tensor.transpose(gz_spread[:], gz_cols[:, LAST : LAST + 1].to_broadcast([P, P]), identity[:])
+        gz_last = held([P, P], F32, "gz_last")
+        nc.scalar.copy(gz_last[:], gz_spread[:])
+
+        sums = {}
+
+        def add_turned(s, term, first=False, last=False):
+            if first:
+                sums[s] = [bank(SUM_BANKS[s] + h, [P, BANK_CHUNKS, P]) for h in range(2)]
+            for h in range(2):
+                for c in range(BANK_CHUNKS):
+                    j0 = CHUNK * (BANK_CHUNKS * h + c)
+                    nc.tensor.matmul(
+                        sums[s][h][:, c, :],
+                        term[:, j0 : j0 + CHUNK],
+                        identity[:],
+                        is_transpose=True,
+                        start=(first and c == 0),
+                        stop=(last and c == BANK_CHUNKS - 1),
+                    )
+
+        def gained(rows, s, name):
+            if s == LAST:
+                return rows
+            scaled = held([P, S], F32, name)
+            nc.scalar.activation(scaled[:], rows[:], ACT.Copy, scale=gz_cols[:, s : s + 1])
+            return scaled
+
+        def sky_turns(s, number):
+            x = bank(number, [P, S])
+            for a in range(2):
+                nc.tensor.matmul_mx(
+                    out=x[:],
+                    lhsT=w2_codes[:, a, 2 * P * s : 2 * P * (s + 1)].bitcast(FP4X4),
+                    lhsT_scale=w2_scale_planes[:, a * H + P * s : a * H + P * (s + 1)],
+                    rhs=sky_codes[a][:].bitcast(FP8X4),
+                    rhs_scale=sky_scales[a][:],
+                    start=(a == 0),
+                    stop=(a == 1),
+                )
+            turns = staged([P, S], F32, "turns", 2)
+            nc.scalar.activation(turns[:], x[:], ACT.Copy, scale=1.0 / (2.0 * math.pi))
+            whole = staged([P, S], U32, "whole", 2)
+            nc.scalar.activation(whole[:], turns[:], ACT.Copy, bias=ROUND)
+            rest = staged([P, S], F32, "rest", 2)
+            nc.vector.scalar_tensor_tensor(
+                rest[:], whole[:].bitcast(I32), ROUND, turns[:], ALU.subtract, ALU.subtract
+            )
+            return rest
+
+        def sky_place(s, rest, h2, page):
+            nc.scalar.activation(h2[:], rest[:], ACT.Sin, scale=-2.0 * math.pi)
+            weights = gained(wg2_rows, s, "wg2_gained%d" % s)
+            nc.vector.tensor_tensor(page[:].indirect(sky_places[:]), h2[:], weights[:], ALU.mult)
+
+        sky_order = [LAST] + list(range(LAST))
+        rests = []
+        for n, s in enumerate(sky_order):
+            rests.append(sky_turns(s, n % 2))
+            if n < LAST:
+                sky_place(s, rests[n], staged([P, S], F32, "h", 3), sky_pages[n % 2])
+                add_turned(s, sky_pages[n % 2], first=True)
+
+        spax_scales = gather(spax_scales_raw[:], spax_list, U8, "spax_scales")
+        spax_codes = [gather(spax_words[a][:], spax_list, U32, "spax_codes%d" % a) for a in range(2)]
+        w1_mx = [quantize(round_plain(w1_raw[a])[:], "w1_%d" % a) for a in range(2)]
+        sky_place(sky_order[LAST], rests[LAST], held([P, S], F32, "h2_last", "w1_raw1"), sky_pages[LAST % 2])
+
+        wd_raw = load_rows(wd, "wd_raw", "w1_raw0")
+        wo_raw = held([P, 2, N], I32, "wo_raw")
+        nc.sync.dma_start(wo_raw[:], wo_words.rearrange("a p c i -> p a (c i)").bitcast(I32))
+        load_scales_stacked(nc.sync, wo_scales_raw, wo_scales)
+
+        def spax_place(s):
+            x = bank(s % 2, [P, S])
+            for a in range(2):
+                nc.tensor.matmul_mx(
+                    out=x[:],
+                    lhsT=w1_mx[a][0][:, P * s : P * (s + 1)].bitcast(FP8X4),
+                    lhsT_scale=w1_mx[a][1][:, P * s : P * (s + 1)],
+                    rhs=spax_codes[a][:].bitcast(FP8X4),
+                    rhs_scale=spax_scales[4 * a :, :],
+                    start=(a == 0),
+                    stop=(a == 1),
+                )
+            h1 = staged([P, S], F32, "h", 3)
+            nc.scalar.activation(h1[:], x[:], ACT.Tanh)
+            weights = gained(wg1_rows, s, "wg1_gained%d" % s)
+            page = spax_pages[s % 2]
+            nc.vector.tensor_tensor(page[:].indirect(spax_places[:]), h1[:], weights[:], ALU.mult)
+            return page
+
+        z_turned = [held([P, BANK_CHUNKS, H], BF16, "z_turned%d" % h) for h in range(2)]
+
+        def gained_template(s):
+            if s != LAST:
+                nc.scalar.activation(tpl_rows[s][:], tpl_rows[s][:], ACT.Copy, scale=gz_cols[:, s : s + 1])
+            return tpl_rows[s]
+
+        def round_turned(s):
+            for h in range(2):
+                target = z_turned[h][:, :, P * s : P * (s + 1)]
+                if s == LAST:
+                    nc.vector.tensor_tensor(
+                        target, sums[s][h][:], gz_last[:].unsqueeze(1).to_broadcast([P, BANK_CHUNKS, P]), ALU.mult
+                    )
+                else:
+                    nc.scalar.copy(target, sums[s][h][:])
+
+        for s in range(2):
+            add_turned(s, spax_place(s))
+        wq_rounded = [round_dealt(wq_raw[a]) for a in range(2)]
+        placed = spax_place(2)
+        for s in range(2):
+            add_turned(s, gained_template(s), last=True)
+            round_turned(s)
+        add_turned(2, sky_pages[LAST % 2], first=True)
+        add_turned(2, placed)
+        add_turned(LAST, gained_template(LAST))
+        placed = spax_place(LAST)
+        add_turned(2, gained_template(2), last=True)
+        round_turned(2)
+        wd_rounded = round_dealt(wd_raw)
+        wq_mx = [quantize(wq_rounded[a][:], "wq_%d" % a) for a in range(2)]
+        add_turned(LAST, placed, last=True)
+        round_turned(LAST)
+
+        def z_group(g, c0, count):
+            back = bank(6 + g % 2, [P, 2, count * CHUNK])
+            for c in range(count):
+                words = z_turned[(c0 + c) // BANK_CHUNKS][:, (c0 + c) % BANK_CHUNKS, :].bitcast(F32)
+                for u in range(2):
+                    nc.tensor.transpose(back[:, u, CHUNK * c : CHUNK * (c + 1)], words[:, u : H // 2 : 2], identity[:])
+            if g == 0:
+                z_rounded = held([P, PACK * count * CHUNK], BF16, "z_first", "w1_raw0")
+            else:
+                z_rounded = staged([P, PACK * count * CHUNK], BF16, "z_rounded", 2)
+            nc.scalar.copy(
+                z_rounded[:].bitcast(F32).rearrange("p (j u) -> p j u", u=2), back[:].rearrange("p u j -> p j u")
+            )
+            codes, scales = quantize(z_rounded[:], "z_%d" % g)
+            return [(codes[:, CHUNK * c : CHUNK * (c + 1)], scales[:, CHUNK * c : CHUNK * (c + 1)]) for c in range(count)]
+
+        def f_sums(c, z_chunk):
+            bent = staged([P, 2, CHUNK, PACK], F32, "bent", 3)
+            for a in range(2):
+                sums = bank(4 - 2 * (c % 2) + a, [P, PACK, CHUNK])
+                for t in range(PACK):
+                    nc.tensor.matmul_mx(
+                        out=sums[:, t, :],
+                        lhsT=wq_mx[a][0][:, P * t : P * (t + 1)].bitcast(FP8X4),
+                        lhsT_scale=wq_mx[a][1][:, P * t : P * (t + 1)],
+                        rhs=z_chunk[0].bitcast(FP8X4),
+                        rhs_scale=z_chunk[1],
+                        start=True,
+                        stop=True,
+                    )
+                nc.scalar.activation(bent[:, a], sums[:].rearrange("p t j -> p j t"), ACT.Tanh)
+            return bent
+
+        def f_round(bent):
+            f_rounded = staged([P, 2, CHUNK, PACK], BF16, "f_rounded", 2)
+            nc.vector.tensor_tensor(
+                f_rounded[:], bent[:], gf_cols[:].unsqueeze(2).to_broadcast([P, 2, CHUNK, PACK]), ALU.mult
+            )
+            return f_rounded
+
+        y_rows = [held([P, PACK, T2 // 2], F32, "y_rows%d" % h, "spax_words%d" % h) for h in range(2)]
+        y_codes = held([P, T2], U32, "y_codes")
+        y_scales = held([P, T2], U8, "y_scales")
+        y_out = out_0.rearrange("(p t) j -> p t j", t=PACK)
+        codes_out = out_1[0].rearrange("p j t -> p (j t)").bitcast(I32)
+
+        def y_sums(c, f_mx, z_chunk):
+            sums = bank(c % 2, [P, PACK, CHUNK])
+            for t in range(PACK):
+                cols = slice(P * t, P * (t + 1))
+                nc.tensor.matmul_mx(
+                    out=sums[:, t, :], lhsT=wd_mx[0][:, cols].bitcast(FP8X4), lhsT_scale=wd_mx[1][:, cols],
+                    rhs=z_chunk[0].bitcast(FP8X4), rhs_scale=z_chunk[1], start=True, stop=False,
+                )
+                for a in range(2):
+                    nc.tensor.matmul_mx(
+                        out=sums[:, t, :],
+                        lhsT=wo_codes[:, a, cols].bitcast(FP8X4),
+                        lhsT_scale=wo_scale_planes[4 * a :, cols],
+                        rhs=f_mx[0][:, CHUNK * a : CHUNK * (a + 1)].bitcast(FP8X4),
+                        rhs_scale=f_mx[1][:, CHUNK * a : CHUNK * (a + 1)],
+                        start=False,
+                        stop=(a == 1),
+                    )
+            j0 = CHUNK * (c % BANK_CHUNKS)
+            rows = y_rows[c // BANK_CHUNKS][:, :, j0 : j0 + CHUNK]
+            nc.scalar.copy(rows, sums[:])
+            y_rounded = staged([P, PACK * CHUNK], BF16, "y_rounded", 3)
+            if c in Y_ON_SCALAR:
+                nc.scalar.copy(
+                    y_rounded[:].rearrange("p (j t) -> p j t", t=PACK), sums[:].rearrange("p t j -> p j t")
+                )
+            else:
+                nc.vector.tensor_copy(
+                    y_rounded[:].rearrange("p (c n t) -> p c t n", n=4, t=PACK),
+                    rows.rearrange("p t (c n) -> p c t n", n=4),
+                )
+            return y_rounded
+
+        def y_planes(c, y_rounded):
+            cols = slice(CHUNK * c, CHUNK * (c + 1))
+            nc.vector.quantize_mx(out=y_codes[:, cols].bitcast(FP8X4), scales=y_scales[:, cols], in_=y_rounded[:])
+            if c % 2 == 1:
+                j0 = CHUNK * ((c - 1) % BANK_CHUNKS)
+                pair = slice(CHUNK * (c - 1), CHUNK * (c + 1))
+                nc.sync.dma_start(y_out[:, :, pair], y_rows[c // BANK_CHUNKS][:, :, j0 : j0 + 2 * CHUNK])
+                nc.sync.dma_start(codes_out[:, pair], y_codes[:, pair].bitcast(I32))
+
+        z_chunks = []
+        for g, count in enumerate(Z_GROUPS):
+            z_chunks.extend(z_group(g, len(z_chunks), count))
+            if g == 0:
+                wd_mx = quantize(wd_rounded[:], "wd")
+                wo_codes = held([P, 2, N], U32, "wo_codes")
+                nc.vector.tensor_copy(
+                    wo_codes[:].bitcast(I32).rearrange("p a (t q) -> p a q t", t=PACK),
+                    wo_raw[:].rearrange("p a (q t) -> p a q t", t=PACK),
+                )
+                wo_scale_planes = held([P, N], U8, "wo_scale_planes")
+                nc.vector.tensor_copy(
+                    wo_scale_planes[:].rearrange("p (t q) -> p q t", t=PACK),
+                    wo_scales_raw[:].rearrange("p (q t) -> p q t", t=PACK),
+                )
+
+        bents, f_roundeds, f_mxs, y_roundeds = {}, {}, {}, {}
+        for step in range(CHUNKS + 4):
+            c = step - 4
+            if 0 <= c < CHUNKS:
+                y_planes(c, y_roundeds[c])
+            c = step - 3
+            if 0 <= c < CHUNKS:
+                y_roundeds[c] = y_sums(c, f_mxs[c], z_chunks[c])
+            c = step - 2
+            if 0 <= c < CHUNKS:
+                f_mxs[c] = quantize(f_roundeds[c][:].rearrange("p a j t -> p (a j t)"), "f", 2)
+            c = step - 1
+            if 0 <= c < CHUNKS:
+                f_roundeds[c] = f_round(bents[c])
+            c = step
+            if c < CHUNKS:
+                bents[c] = f_sums(c, z_chunks[c])
+
+        for q in range(QUADS):
+            nc.sync.dma_start(out_2[0, 4 * q : 4 * q + 4, :].bitcast(I32), y_scales[32 * q : 32 * q + 4, :].bitcast(I32))

@@ -121,6 +121,9 @@ def tile_list_spaxel_sky_kinematics_kernel(
         nc.gpsimd.memset(spax_scales_raw[:].bitcast(I32), 0)
         wo_scales_raw = held([P, N], U8, "wo_scales_raw")
         nc.gpsimd.memset(wo_scales_raw[:].bitcast(I32), 0)
+        warm = held([P, 1], F32, "warm")
+        nc.vector.memset(warm[:], 0.0)
+        nc.scalar.activation(warm[:], warm[:], ACT.Silu)
 
         sky_list = load_list(offs2, "sky_list")
         sky_places = load_list(offs4, "sky_places")

@@ -27,8 +27,12 @@ CHUNK = 128
 CHUNKS = T2 // CHUNK
 BANK_CHUNKS = 4
 Z_GROUPS = (1,1,2,2,2,)
-Y_ON_SCALAR = (1,3,5,6,7,)
+Y_ON_SCALAR = (1,3,5,)
 SUM_BANKS = (4, 6, 4, 2)
+HALVES = (slice(0, S // 2), slice(S // 2, S))
+WHOLE = slice(0, S)
+F_PARTS = ((slice(0, 2),), (slice(0, 1), slice(1, 2)))
+LAST_ROUNDS = ((0, 1), (1, 3), (4, 4))
 ROUND = 1.5 * 2.0**23
 
 
@@ -80,6 +84,9 @@ def tile_list_spaxel_sky_kinematics_kernel(
             nc.sync.dma_start(tile[:], rows.rearrange("(p i) c -> p i c", i=PACK))
             return tile
 
+        def entries(offsets, part):
+            return offsets[:, part.start // 16 : part.stop // 16]
+
         def gather(window, offsets, dtype, name):
             picked = held([P, S], dtype, name)
             nc.vector.tensor_copy(picked[:], window.indirect(offsets[:]))
@@ -129,25 +136,25 @@ def tile_list_spaxel_sky_kinematics_kernel(
         sky_places = load_list(offs4, "sky_places")
         spax_list = load_list(offs, "spax_list")
         spax_places = load_list(offs3, "spax_places")
-        gz_cols = held([P, SLOTS], F32, "gz_cols")
-        with nc.allow_non_contiguous_dma(reason="one gain a partition and slot"):
-            nc.sync.dma_start(gz_cols[:], gz.rearrange("(s p) -> p s", p=P))
         gf_cols = held([P, 2, PACK], F32, "gf_cols")
         nc.sync.dma_start(gf_cols[:], gf.rearrange("(a p t) -> p a t", a=2, t=PACK))
         sky_words = [load_words(tab2_words, 0, "sky_words0")]
-        w2_codes = held([P, 2, 2 * H], U8, "w2_codes")
-        nc.sync.dma_start(w2_codes[:].bitcast(I32), w2_words.rearrange("a p c -> p a c").bitcast(I32))
-        load_scales_side_by_side(nc.sync, sky_scales_raw, tab2_scales)
-        sky_words.append(load_words(tab2_words, 1, "sky_words1"))
-        load_scales_side_by_side(nc.sync, w2_scale_planes, w2_scales)
-        spax_words = [load_words(tab_words, 0, "spax_words0")]
+        gz_cols = held([P, SLOTS], F32, "gz_cols")
+        with nc.allow_non_contiguous_dma(reason="one gain a partition and slot"):
+            nc.sync.dma_start(gz_cols[:], gz.rearrange("(s p) -> p s", p=P))
         wg2_rows = held([P, S], F32, "wg2_rows")
         nc.sync.dma_start(wg2_rows[:], wg2)
+        load_scales_side_by_side(nc.sync, sky_scales_raw, tab2_scales)
+        sky_words.append(load_words(tab2_words, 1, "sky_words1"))
+        w2_codes = held([P, 2, 2 * H], U8, "w2_codes")
+        nc.sync.dma_start(w2_codes[:].bitcast(I32), w2_words.rearrange("a p c -> p a c").bitcast(I32))
+        load_scales_side_by_side(nc.sync, w2_scale_planes, w2_scales)
+        spax_words = [load_words(tab_words, 0, "spax_words0")]
         load_scales_stacked(nc.sync, spax_scales_raw, tab_scales)
         spax_words.append(load_words(tab_words, 1, "spax_words1"))
-        w1_raw = [load_rows(w1[512 * a : 512 * (a + 1), :], "w1_raw%d" % a, "w1_raw%d" % a) for a in range(2)]
         wg1_rows = held([P, S], F32, "wg1_rows")
         nc.sync.dma_start(wg1_rows[:], wg1)
+        w1_raw = [load_rows(w1[512 * a : 512 * (a + 1), :], "w1_raw%d" % a, "w1_raw%d" % a) for a in range(2)]
 
         identity = held([P, P], F32, "identity")
         make_identity(nc, identity[:])
@@ -156,7 +163,9 @@ def tile_list_spaxel_sky_kinematics_kernel(
         sky_scales = [
             gather(sky_scales_raw[:, a * T : (a + 1) * T], sky_list, U8, "sky_scales%d" % a) for a in range(2)
         ]
-        sky_codes.append(gather(sky_words[1][:], sky_list, U32, "sky_codes1"))
+        sky_codes.append(held([P, S], U32, "sky_codes1"))
+        for part in HALVES:
+            nc.vector.tensor_copy(sky_codes[1][:, part], sky_words[1][:].indirect(entries(sky_list, part)))
 
         wq_raw = [load_rows(wq[:, 512 * a : 512 * (a + 1)], "wq_raw%d" % a, "sky_words%d" % a) for a in range(2)]
         tpl_rows = []
@@ -199,45 +208,50 @@ def tile_list_spaxel_sky_kinematics_kernel(
             nc.scalar.activation(scaled[:], rows[:], ACT.Copy, scale=gz_cols[:, s : s + 1])
             return scaled
 
-        def sky_turns(s, number):
-            x = bank(number, [P, S])
+        def sky_turns(s, number, part):
+            width = part.stop - part.start
+            x = bank(number, [P, width])
             for a in range(2):
                 nc.tensor.matmul_mx(
                     out=x[:],
                     lhsT=w2_codes[:, a, 2 * P * s : 2 * P * (s + 1)].bitcast(FP4X4),
                     lhsT_scale=w2_scale_planes[:, a * H + P * s : a * H + P * (s + 1)],
-                    rhs=sky_codes[a][:].bitcast(FP8X4),
-                    rhs_scale=sky_scales[a][:],
+                    rhs=sky_codes[a][:, part].bitcast(FP8X4),
+                    rhs_scale=sky_scales[a][:, part],
                     start=(a == 0),
                     stop=(a == 1),
                 )
-            turns = staged([P, S], F32, "turns", 2)
+            turns = staged([P, width], F32, "turns", 2)
             nc.scalar.activation(turns[:], x[:], ACT.Copy, scale=1.0 / (2.0 * math.pi))
-            whole = staged([P, S], U32, "whole", 2)
+            whole = staged([P, width], U32, "whole", 2)
             nc.scalar.activation(whole[:], turns[:], ACT.Copy, bias=ROUND)
-            rest = staged([P, S], F32, "rest", 2)
+            rest = staged([P, width], F32, "rest", 2)
             nc.vector.scalar_tensor_tensor(
                 rest[:], whole[:].bitcast(I32), ROUND, turns[:], ALU.subtract, ALU.subtract
             )
             return rest
 
-        def sky_place(s, rest, h2, page):
+        def sky_place(rest, h2, weights, page, part):
             nc.scalar.activation(h2[:], rest[:], ACT.Sin, scale=-2.0 * math.pi)
-            weights = gained(wg2_rows, s, "wg2_gained%d" % s)
-            nc.vector.tensor_tensor(page[:].indirect(sky_places[:]), h2[:], weights[:], ALU.mult)
+            nc.vector.tensor_tensor(
+                page[:].indirect(entries(sky_places, part)), h2[:], weights[:, part], ALU.mult
+            )
 
-        sky_order = [LAST] + list(range(LAST))
-        rests = []
-        for n, s in enumerate(sky_order):
-            rests.append(sky_turns(s, n % 2))
-            if n < LAST:
-                sky_place(s, rests[n], staged([P, S], F32, "h", 3), sky_pages[n % 2])
-                add_turned(s, sky_pages[n % 2], first=True)
+        wg2_gained = [gained(wg2_rows, s, "wg2_gained%d" % s) for s in range(SLOTS)]
+        for n, part in enumerate(HALVES):
+            rest = sky_turns(LAST, n, part)
+            sky_place(rest, staged([P, S // 2], F32, "h", 3), wg2_gained[LAST], sky_pages[0], part)
+        add_turned(LAST, sky_pages[0], first=True)
+        for s in range(2):
+            rest = sky_turns(s, s, WHOLE)
+            sky_place(rest, staged([P, S], F32, "h", 3), wg2_gained[s], sky_pages[1 - s], WHOLE)
+            add_turned(s, sky_pages[1 - s], first=True)
+        rest = sky_turns(2, 0, WHOLE)
 
         spax_scales = gather(spax_scales_raw[:], spax_list, U8, "spax_scales")
         spax_codes = [gather(spax_words[a][:], spax_list, U32, "spax_codes%d" % a) for a in range(2)]
         w1_mx = [quantize(round_plain(w1_raw[a])[:], "w1_%d" % a) for a in range(2)]
-        sky_place(sky_order[LAST], rests[LAST], held([P, S], F32, "h2_last", "w1_raw1"), sky_pages[LAST % 2])
+        sky_place(rest, held([P, S], F32, "h2_last", "w1_raw1"), wg2_gained[2], sky_pages[1], WHOLE)
 
         wd_raw = load_rows(wd, "wd_raw", "w1_raw0")
         wo_raw = held([P, 2, N], I32, "wo_raw")
@@ -272,13 +286,16 @@ def tile_list_spaxel_sky_kinematics_kernel(
 
         def round_turned(s):
             for h in range(2):
-                target = z_turned[h][:, :, P * s : P * (s + 1)]
-                if s == LAST:
-                    nc.vector.tensor_tensor(
-                        target, sums[s][h][:], gz_last[:].unsqueeze(1).to_broadcast([P, BANK_CHUNKS, P]), ALU.mult
-                    )
-                else:
-                    nc.scalar.copy(target, sums[s][h][:])
+                nc.scalar.copy(z_turned[h][:, :, P * s : P * (s + 1)], sums[s][h][:])
+
+        def round_last_turned(first, count):
+            h, c = divmod(first, BANK_CHUNKS)
+            nc.vector.tensor_tensor(
+                z_turned[h][:, c : c + count, P * LAST :],
+                sums[LAST][h][:, c : c + count, :],
+                gz_last[:].unsqueeze(1).to_broadcast([P, count, P]),
+                ALU.mult,
+            )
 
         for s in range(2):
             add_turned(s, spax_place(s))
@@ -287,16 +304,18 @@ def tile_list_spaxel_sky_kinematics_kernel(
         for s in range(2):
             add_turned(s, gained_template(s), last=True)
             round_turned(s)
-        add_turned(2, sky_pages[LAST % 2], first=True)
-        add_turned(2, placed)
+        add_turned(2, sky_pages[1], first=True)
+        add_turned(2, gained_template(2))
         add_turned(LAST, gained_template(LAST))
+        add_turned(2, placed, last=True)
         placed = spax_place(LAST)
-        add_turned(2, gained_template(2), last=True)
         round_turned(2)
         wd_rounded = round_dealt(wd_raw)
-        wq_mx = [quantize(wq_rounded[a][:], "wq_%d" % a) for a in range(2)]
         add_turned(LAST, placed, last=True)
-        round_turned(LAST)
+
+        wq_codes = held([P, 2, 512], U32, "wq_codes", "wg1_rows")
+        wq_scales = held([P, 2, 512], U8, "wq_scales")
+        wq_mx = [(wq_codes[:, a, :], wq_scales[:, a, :]) for a in range(2)]
 
         def z_group(g, c0, count):
             back = bank(6 + g % 2, [P, 2, count * CHUNK])
@@ -315,7 +334,7 @@ def tile_list_spaxel_sky_kinematics_kernel(
             return [(codes[:, CHUNK * c : CHUNK * (c + 1)], scales[:, CHUNK * c : CHUNK * (c + 1)]) for c in range(count)]
 
         def f_sums(c, z_chunk):
-            bent = staged([P, 2, CHUNK, PACK], F32, "bent", 3)
+            bent = staged([P, 2, CHUNK, PACK], F32, "bent", 5)
             for a in range(2):
                 sums = bank(4 - 2 * (c % 2) + a, [P, PACK, CHUNK])
                 for t in range(PACK):
@@ -331,14 +350,26 @@ def tile_list_spaxel_sky_kinematics_kernel(
                 nc.scalar.activation(bent[:, a], sums[:].rearrange("p t j -> p j t"), ACT.Tanh)
             return bent
 
-        def f_round(bent):
+        def f_round(c, bent):
             f_rounded = staged([P, 2, CHUNK, PACK], BF16, "f_rounded", 2)
-            nc.vector.tensor_tensor(
-                f_rounded[:], bent[:], gf_cols[:].unsqueeze(2).to_broadcast([P, 2, CHUNK, PACK]), ALU.mult
-            )
+            for part in F_PARTS[c in (0, CHUNKS - 1)]:
+                shape = [P, part.stop - part.start, CHUNK, PACK]
+                nc.vector.tensor_tensor(
+                    f_rounded[:, part], bent[:, part], gf_cols[:, part].unsqueeze(2).to_broadcast(shape), ALU.mult
+                )
             return f_rounded
 
+        def f_quantize(c, f_rounded):
+            operands = []
+            for part in F_PARTS[c in (0, CHUNKS - 1)]:
+                codes, scales = quantize(f_rounded[:, part].rearrange("p a j t -> p (a j t)"), "f", 3)
+                for a in range(part.stop - part.start):
+                    cols = slice(CHUNK * a, CHUNK * (a + 1))
+                    operands.append((codes[:, cols], scales[:, cols]))
+            return operands
+
         y_rows = [held([P, PACK, T2 // 2], F32, "y_rows%d" % h, "spax_words%d" % h) for h in range(2)]
+        y_rounded = [held([P, T2 // 2, PACK], BF16, "y_rounded%d" % h) for h in range(2)]
         y_codes = held([P, T2], U32, "y_codes")
         y_scales = held([P, T2], U8, "y_scales")
         y_out = out_0.rearrange("(p t) j -> p t j", t=PACK)
@@ -346,50 +377,61 @@ def tile_list_spaxel_sky_kinematics_kernel(
 
         def y_sums(c, f_mx, z_chunk):
             sums = bank(c % 2, [P, PACK, CHUNK])
-            for t in range(PACK):
-                cols = slice(P * t, P * (t + 1))
-                nc.tensor.matmul_mx(
-                    out=sums[:, t, :], lhsT=wd_mx[0][:, cols].bitcast(FP8X4), lhsT_scale=wd_mx[1][:, cols],
-                    rhs=z_chunk[0].bitcast(FP8X4), rhs_scale=z_chunk[1], start=True, stop=False,
-                )
-                for a in range(2):
+            passes = [(wd_mx[0][:], wd_mx[1][:], z_chunk)]
+            passes.extend((wo_codes[:, a, :], wo_scale_planes[4 * a :, :], f_mx[a]) for a in range(2))
+            for n, (codes, scales, moving) in enumerate(passes):
+                for t in range(PACK):
+                    cols = slice(P * t, P * (t + 1))
                     nc.tensor.matmul_mx(
                         out=sums[:, t, :],
-                        lhsT=wo_codes[:, a, cols].bitcast(FP8X4),
-                        lhsT_scale=wo_scale_planes[4 * a :, cols],
-                        rhs=f_mx[0][:, CHUNK * a : CHUNK * (a + 1)].bitcast(FP8X4),
-                        rhs_scale=f_mx[1][:, CHUNK * a : CHUNK * (a + 1)],
-                        start=False,
-                        stop=(a == 1),
+                        lhsT=codes[:, cols].bitcast(FP8X4),
+                        lhsT_scale=scales[:, cols],
+                        rhs=moving[0].bitcast(FP8X4),
+                        rhs_scale=moving[1],
+                        start=(n == 0 and t == 0),
+                        stop=(n == len(passes) - 1 and t == PACK - 1),
                     )
             j0 = CHUNK * (c % BANK_CHUNKS)
             rows = y_rows[c // BANK_CHUNKS][:, :, j0 : j0 + CHUNK]
             nc.scalar.copy(rows, sums[:])
-            y_rounded = staged([P, PACK * CHUNK], BF16, "y_rounded", 3)
             if c in Y_ON_SCALAR:
                 nc.scalar.copy(
-                    y_rounded[:].rearrange("p (j t) -> p j t", t=PACK), sums[:].rearrange("p t j -> p j t")
+                    y_rounded[c // BANK_CHUNKS][:, j0 : j0 + CHUNK, :], sums[:].rearrange("p t j -> p j t")
                 )
-            else:
-                nc.vector.tensor_copy(
-                    y_rounded[:].rearrange("p (c n t) -> p c t n", n=4, t=PACK),
-                    rows.rearrange("p t (c n) -> p c t n", n=4),
+            if c % 2 == 1 or c == CHUNKS - 2:
+                first = c - 1 if c < CHUNKS - 2 else c
+                nc.sync.dma_start(
+                    y_out[:, :, CHUNK * first : CHUNK * (c + 1)],
+                    y_rows[c // BANK_CHUNKS][:, :, CHUNK * (first % BANK_CHUNKS) : j0 + CHUNK],
                 )
-            return y_rounded
 
-        def y_planes(c, y_rounded):
-            cols = slice(CHUNK * c, CHUNK * (c + 1))
-            nc.vector.quantize_mx(out=y_codes[:, cols].bitcast(FP8X4), scales=y_scales[:, cols], in_=y_rounded[:])
-            if c % 2 == 1:
-                j0 = CHUNK * ((c - 1) % BANK_CHUNKS)
-                pair = slice(CHUNK * (c - 1), CHUNK * (c + 1))
-                nc.sync.dma_start(y_out[:, :, pair], y_rows[c // BANK_CHUNKS][:, :, j0 : j0 + 2 * CHUNK])
-                nc.sync.dma_start(codes_out[:, pair], y_codes[:, pair].bitcast(I32))
+        def y_planes(first, count):
+            half = first // BANK_CHUNKS
+            for c in range(first, first + count):
+                if c not in Y_ON_SCALAR:
+                    cols = slice(CHUNK * (c % BANK_CHUNKS), CHUNK * (c % BANK_CHUNKS + 1))
+                    nc.vector.tensor_copy(
+                        y_rounded[half][:, cols, :].rearrange("p (c n) t -> p c t n", n=4),
+                        y_rows[half][:, :, cols].rearrange("p t (c n) -> p c t n", n=4),
+                    )
+            j0 = CHUNK * (first % BANK_CHUNKS)
+            cols = slice(CHUNK * first, CHUNK * (first + count))
+            nc.vector.quantize_mx(
+                out=y_codes[:, cols].bitcast(FP8X4),
+                scales=y_scales[:, cols],
+                in_=y_rounded[half][:, j0 : j0 + CHUNK * count, :].rearrange("p j t -> p (j t)"),
+            )
+            nc.sync.dma_start(codes_out[:, cols], y_codes[:, cols].bitcast(I32))
 
         z_chunks = []
         for g, count in enumerate(Z_GROUPS):
+            if g < len(LAST_ROUNDS):
+                round_last_turned(*LAST_ROUNDS[g])
             z_chunks.extend(z_group(g, len(z_chunks), count))
             if g == 0:
+                for a in range(2):
+                    nc.vector.quantize_mx(out=wq_mx[a][0].bitcast(FP8X4), scales=wq_mx[a][1], in_=wq_rounded[a][:])
+            if g == 2:
                 wd_mx = quantize(wd_rounded[:], "wd")
                 wo_codes = held([P, 2, N], U32, "wo_codes")
                 nc.vector.tensor_copy(
@@ -402,23 +444,23 @@ def tile_list_spaxel_sky_kinematics_kernel(
                     wo_scales_raw[:].rearrange("p (q t) -> p q t", t=PACK),
                 )
 
-        bents, f_roundeds, f_mxs, y_roundeds = {}, {}, {}, {}
-        for step in range(CHUNKS + 4):
-            c = step - 4
-            if 0 <= c < CHUNKS:
-                y_planes(c, y_roundeds[c])
+        bents, f_roundeds, f_mxs = {}, {}, {}
+        for step in range(CHUNKS + 3):
             c = step - 3
             if 0 <= c < CHUNKS:
-                y_roundeds[c] = y_sums(c, f_mxs[c], z_chunks[c])
+                y_sums(c, f_mxs[c], z_chunks[c])
             c = step - 2
             if 0 <= c < CHUNKS:
-                f_mxs[c] = quantize(f_roundeds[c][:].rearrange("p a j t -> p (a j t)"), "f", 2)
+                f_mxs[c] = f_quantize(c, f_roundeds[c])
             c = step - 1
             if 0 <= c < CHUNKS:
-                f_roundeds[c] = f_round(bents[c])
+                f_roundeds[c] = f_round(c, bents[c])
             c = step
             if c < CHUNKS:
                 bents[c] = f_sums(c, z_chunks[c])
+
+        for first, count in ((0, 4), (4, 3), (7, 1)):
+            y_planes(first, count)
 
         for q in range(QUADS):
             nc.sync.dma_start(out_2[0, 4 * q : 4 * q + 4, :].bitcast(I32), y_scales[32 * q : 32 * q + 4, :].bitcast(I32))

@@ -27,7 +27,7 @@ CHUNK = 128
 CHUNKS = T2 // CHUNK
 BANK_CHUNKS = 4
 Z_GROUPS = (1,1,2,2,2,)
-Y_ON_SCALAR = (1,3,5,)
+Y_ON_SCALAR = ()
 SUM_BANKS = (4, 6, 4, 2)
 HALVES = (slice(0, S // 2), slice(S // 2, S))
 WHOLE = slice(0, S)
@@ -117,7 +117,7 @@ def tile_list_spaxel_sky_kinematics_kernel(
             dealt = rounded[:].rearrange("p (t q i) -> p q i t", t=PACK, i=PACK)
             source = raw[:].rearrange("p i (q t) -> p q i t", t=PACK)
             for half in range(2):
-                nc.scalar.copy(dealt[:, 64 * half : 64 * (half + 1)], source[:, 64 * half : 64 * (half + 1)])
+                nc.scalar.copy(dealt[:, :, :, 2 * half : 2 * half + 2], source[:, :, :, 2 * half : 2 * half + 2])
             return rounded
 
         sky_scales_raw = held([P, 2 * T], U8, "sky_scales_raw")
@@ -440,8 +440,8 @@ def tile_list_spaxel_sky_kinematics_kernel(
                 )
                 wo_scale_planes = held([P, N], U8, "wo_scale_planes")
                 nc.vector.tensor_copy(
-                    wo_scale_planes[:].rearrange("p (t q) -> p q t", t=PACK),
-                    wo_scales_raw[:].rearrange("p (q t) -> p q t", t=PACK),
+                    wo_scale_planes[:].rearrange("p (t q) -> p t q", t=PACK),
+                    wo_scales_raw[:].rearrange("p (q t) -> p t q", t=PACK),
                 )
 
         bents, f_roundeds, f_mxs = {}, {}, {}

@@ -20,19 +20,30 @@ ACT = mybir.ActivationFunctionType
 
 P = 128
 PACK = 4
+PASS = P * PACK
 QUADS = 4
+STRIPE = 16
+LINE = 4
 SLOTS = H // P
 LAST = SLOTS - 1
 CHUNK = 128
 CHUNKS = T2 // CHUNK
 BANK_CHUNKS = 4
-Z_GROUPS = (1,1,2,2,2,)
-Y_ON_SCALAR = ()
+PAIRS = P // PACK
+
 SUM_BANKS = (4, 6, 4, 2)
+BACK_BANK = 6
+F_BANKS = (4, 2)
+
 HALVES = (slice(0, S // 2), slice(S // 2, S))
 WHOLE = slice(0, S)
-F_PARTS = ((slice(0, 2),), (slice(0, 1), slice(1, 2)))
-LAST_ROUNDS = ((0, 1), (1, 3), (4, 4))
+LAST_ROUNDS = ((0, 1), (1, BANK_CHUNKS - 1), (BANK_CHUNKS, BANK_CHUNKS))
+Z_GROUPS = (1, 1, 2, 2, 2)
+EARLY_F = 2
+BOTH_PASSES = (slice(0, 2),)
+PASS_BY_PASS = (slice(0, 1), slice(1, 2))
+PLANE_CALLS = ((0, BANK_CHUNKS), (BANK_CHUNKS, BANK_CHUNKS - 1), (CHUNKS - 1, 1))
+ROUNDED_BUFS, BENT_BUFS, H_BUFS, F_BUFS = 3, 5, 3, 3
 ROUND = 1.5 * 2.0**23
 
 
@@ -47,17 +58,17 @@ def tile_list_spaxel_sky_kinematics_kernel(
         ring = ctx.enter_context(tc.tile_pool(name="ring", bufs=2))
         psum = ctx.enter_context(tc.psum_pool(name="psum", bufs=1))
 
-        def held(shape, dtype, name, tag=None):
-            return keep.tile(shape, dtype, name=name, tag=tag or name, align_bytes=64)
+        def held(shape, dtype, name, after=None):
+            return keep.tile(shape, dtype, name=name, tag=after or name, align_bytes=64)
 
-        def staged(shape, dtype, name, bufs):
+        def staged(shape, dtype, name, bufs=2):
             return ring.tile(shape, dtype, name=name, tag=name, bufs=bufs, align_bytes=64)
 
         def bank(number, shape):
             return psum.tile(shape, F32, name="bank%d" % number, tag="bank%d" % number)
 
         def load_list(source, name):
-            tile = lists.tile([P, S // 16], U16, name=name)
+            tile = lists.tile([P, S // STRIPE], U16, name=name)
             nc.sync.dma_start(tile[:], source)
             return tile
 
@@ -66,59 +77,59 @@ def tile_list_spaxel_sky_kinematics_kernel(
             nc.sync.dma_start(tile[:].bitcast(I32), words[a].rearrange("p t i -> p (t i)").bitcast(I32))
             return tile
 
-        def load_scales_side_by_side(queue, tile, scales):
+        def load_scales_side_by_side(tile, scales):
             for q in range(QUADS):
-                queue.dma_start(
+                nc.sync.dma_start(
                     tile[32 * q : 32 * q + 4, :].bitcast(I32).rearrange("r (a w) -> r a w", a=2),
                     scales[:, 4 * q : 4 * q + 4, :].rearrange("a r c -> r a c").bitcast(I32),
                 )
 
-        def load_scales_stacked(queue, tile, scales):
+        def load_scales_stacked(tile, scales):
             for q in range(QUADS):
-                queue.dma_start(
+                nc.sync.dma_start(
                     tile[32 * q : 32 * q + 8, :].bitcast(I32), scales[:, 4 * q : 4 * q + 4, :].bitcast(I32)
                 )
 
-        def load_rows(rows, name, tag):
-            tile = held([P, PACK, rows.shape[1]], F32, name, tag)
+        def load_rows(rows, name, after=None):
+            tile = held([P, PACK, rows.shape[1]], F32, name, after)
             nc.sync.dma_start(tile[:], rows.rearrange("(p i) c -> p i c", i=PACK))
             return tile
 
         def entries(offsets, part):
-            return offsets[:, part.start // 16 : part.stop // 16]
+            return offsets[:, part.start // STRIPE : part.stop // STRIPE]
 
         def gather(window, offsets, dtype, name):
             picked = held([P, S], dtype, name)
             nc.vector.tensor_copy(picked[:], window.indirect(offsets[:]))
             return picked
 
-        def quantize(rounded, name, bufs=None):
-            width = rounded.shape[1] // PACK
-            if bufs is None:
-                codes = held([P, width], U32, name + "_codes")
-                scales = held([P, width], U8, name + "_scales")
-            else:
-                codes = staged([P, width], U32, name + "_codes", bufs)
-                scales = staged([P, width], U8, name + "_scales", bufs)
-            nc.vector.quantize_mx(out=codes[:].bitcast(FP8X4), scales=scales[:], in_=rounded)
+        def quantize(rounded, codes, scales):
+            nc.vector.quantize_mx(out=codes.bitcast(FP8X4), scales=scales, in_=rounded)
             return codes, scales
 
+        def quantize_held(rounded, name):
+            width = rounded.shape[1] // PACK
+            codes = held([P, width], U32, name + "_codes")
+            scales = held([P, width], U8, name + "_scales")
+            return quantize(rounded, codes[:], scales[:])
+
         def round_plain(raw):
-            rounded = staged([P, PACK * 512], BF16, "rounded", 3)
+            rounded = staged([P, PASS, PACK], BF16, "rounded", ROUNDED_BUFS)
             for half in range(2):
+                cols = slice(PASS // 2 * half, PASS // 2 * (half + 1))
                 nc.scalar.copy(
-                    rounded[:, 1024 * half : 1024 * (half + 1)].rearrange("p (c n i) -> p c i n", n=4, i=PACK),
-                    raw[:, :, 256 * half : 256 * (half + 1)].rearrange("p i (c n) -> p c i n", n=4),
+                    rounded[:, cols, :].rearrange("p (c n) i -> p c i n", n=LINE),
+                    raw[:, :, cols].rearrange("p i (c n) -> p c i n", n=LINE),
                 )
-            return rounded
+            return rounded[:].rearrange("p c i -> p (c i)")
 
         def round_dealt(raw):
-            rounded = staged([P, PACK * 512], BF16, "rounded", 3)
-            dealt = rounded[:].rearrange("p (t q i) -> p q i t", t=PACK, i=PACK)
+            rounded = staged([P, PASS, PACK], BF16, "rounded", ROUNDED_BUFS)
+            dealt = rounded[:].rearrange("p (t q) i -> p q i t", t=PACK)
             source = raw[:].rearrange("p i (q t) -> p q i t", t=PACK)
             for half in range(2):
                 nc.scalar.copy(dealt[:, :, :, 2 * half : 2 * half + 2], source[:, :, :, 2 * half : 2 * half + 2])
-            return rounded
+            return rounded[:].rearrange("p c i -> p (c i)")
 
         sky_scales_raw = held([P, 2 * T], U8, "sky_scales_raw")
         nc.vector.memset(sky_scales_raw[:].bitcast(I32), 0)
@@ -144,17 +155,17 @@ def tile_list_spaxel_sky_kinematics_kernel(
             nc.sync.dma_start(gz_cols[:], gz.rearrange("(s p) -> p s", p=P))
         wg2_rows = held([P, S], F32, "wg2_rows")
         nc.sync.dma_start(wg2_rows[:], wg2)
-        load_scales_side_by_side(nc.sync, sky_scales_raw, tab2_scales)
+        load_scales_side_by_side(sky_scales_raw, tab2_scales)
         sky_words.append(load_words(tab2_words, 1, "sky_words1"))
         w2_codes = held([P, 2, 2 * H], U8, "w2_codes")
         nc.sync.dma_start(w2_codes[:].bitcast(I32), w2_words.rearrange("a p c -> p a c").bitcast(I32))
-        load_scales_side_by_side(nc.sync, w2_scale_planes, w2_scales)
+        load_scales_side_by_side(w2_scale_planes, w2_scales)
         spax_words = [load_words(tab_words, 0, "spax_words0")]
-        load_scales_stacked(nc.sync, spax_scales_raw, tab_scales)
+        load_scales_stacked(spax_scales_raw, tab_scales)
         spax_words.append(load_words(tab_words, 1, "spax_words1"))
         wg1_rows = held([P, S], F32, "wg1_rows")
         nc.sync.dma_start(wg1_rows[:], wg1)
-        w1_raw = [load_rows(w1[512 * a : 512 * (a + 1), :], "w1_raw%d" % a, "w1_raw%d" % a) for a in range(2)]
+        w1_raw = [load_rows(w1[PASS * a : PASS * (a + 1), :], "w1_raw%d" % a) for a in range(2)]
 
         identity = held([P, P], F32, "identity")
         make_identity(nc, identity[:])
@@ -167,7 +178,7 @@ def tile_list_spaxel_sky_kinematics_kernel(
         for part in HALVES:
             nc.vector.tensor_copy(sky_codes[1][:, part], sky_words[1][:].indirect(entries(sky_list, part)))
 
-        wq_raw = [load_rows(wq[:, 512 * a : 512 * (a + 1)], "wq_raw%d" % a, "sky_words%d" % a) for a in range(2)]
+        wq_raw = [load_rows(wq[:, PASS * a : PASS * (a + 1)], "wq_raw%d" % a, "sky_words%d" % a) for a in range(2)]
         tpl_rows = []
         for s in range(SLOTS):
             rows = held([P, T2], F32, "tpl_rows%d" % s)
@@ -181,19 +192,22 @@ def tile_list_spaxel_sky_kinematics_kernel(
 
         gz_spread = bank(0, [P, P])
         nc.tensor.transpose(gz_spread[:], gz_cols[:, LAST : LAST + 1].to_broadcast([P, P]), identity[:])
-        gz_last = held([P, P], F32, "gz_last")
-        nc.scalar.copy(gz_last[:], gz_spread[:])
+        gz_last = held([P, 2, 2 * PAIRS], F32, "gz_last")
+        nc.scalar.copy(
+            gz_last[:].rearrange("j u (p e) -> j u p e", e=2),
+            gz_spread[:].rearrange("j (p u e) -> j u p e", u=2, e=2),
+        )
 
-        sums = {}
+        z_sums = {}
 
         def add_turned(s, term, first=False, last=False):
             if first:
-                sums[s] = [bank(SUM_BANKS[s] + h, [P, BANK_CHUNKS, P]) for h in range(2)]
+                z_sums[s] = [bank(SUM_BANKS[s] + h, [P, BANK_CHUNKS, P]) for h in range(2)]
             for h in range(2):
                 for c in range(BANK_CHUNKS):
                     j0 = CHUNK * (BANK_CHUNKS * h + c)
                     nc.tensor.matmul(
-                        sums[s][h][:, c, :],
+                        z_sums[s][h][:, c, :],
                         term[:, j0 : j0 + CHUNK],
                         identity[:],
                         is_transpose=True,
@@ -208,12 +222,12 @@ def tile_list_spaxel_sky_kinematics_kernel(
             nc.scalar.activation(scaled[:], rows[:], ACT.Copy, scale=gz_cols[:, s : s + 1])
             return scaled
 
-        def sky_turns(s, number, part):
+        def sky_rest(s, number, part):
             width = part.stop - part.start
-            x = bank(number, [P, width])
+            angle = bank(number, [P, width])
             for a in range(2):
                 nc.tensor.matmul_mx(
-                    out=x[:],
+                    out=angle[:],
                     lhsT=w2_codes[:, a, 2 * P * s : 2 * P * (s + 1)].bitcast(FP4X4),
                     lhsT_scale=w2_scale_planes[:, a * H + P * s : a * H + P * (s + 1)],
                     rhs=sky_codes[a][:, part].bitcast(FP8X4),
@@ -221,11 +235,11 @@ def tile_list_spaxel_sky_kinematics_kernel(
                     start=(a == 0),
                     stop=(a == 1),
                 )
-            turns = staged([P, width], F32, "turns", 2)
-            nc.scalar.activation(turns[:], x[:], ACT.Copy, scale=1.0 / (2.0 * math.pi))
-            whole = staged([P, width], U32, "whole", 2)
+            turns = staged([P, width], F32, "turns")
+            nc.scalar.activation(turns[:], angle[:], ACT.Copy, scale=1.0 / (2.0 * math.pi))
+            whole = staged([P, width], U32, "whole")
             nc.scalar.activation(whole[:], turns[:], ACT.Copy, bias=ROUND)
-            rest = staged([P, width], F32, "rest", 2)
+            rest = staged([P, width], F32, "rest")
             nc.vector.scalar_tensor_tensor(
                 rest[:], whole[:].bitcast(I32), ROUND, turns[:], ALU.subtract, ALU.subtract
             )
@@ -239,30 +253,30 @@ def tile_list_spaxel_sky_kinematics_kernel(
 
         wg2_gained = [gained(wg2_rows, s, "wg2_gained%d" % s) for s in range(SLOTS)]
         for n, part in enumerate(HALVES):
-            rest = sky_turns(LAST, n, part)
-            sky_place(rest, staged([P, S // 2], F32, "h", 3), wg2_gained[LAST], sky_pages[0], part)
+            rest = sky_rest(LAST, n, part)
+            sky_place(rest, staged([P, S // 2], F32, "h", H_BUFS), wg2_gained[LAST], sky_pages[0], part)
         add_turned(LAST, sky_pages[0], first=True)
         for s in range(2):
-            rest = sky_turns(s, s, WHOLE)
-            sky_place(rest, staged([P, S], F32, "h", 3), wg2_gained[s], sky_pages[1 - s], WHOLE)
+            rest = sky_rest(s, s, WHOLE)
+            sky_place(rest, staged([P, S], F32, "h", H_BUFS), wg2_gained[s], sky_pages[1 - s], WHOLE)
             add_turned(s, sky_pages[1 - s], first=True)
-        rest = sky_turns(2, 0, WHOLE)
+        rest = sky_rest(2, 0, WHOLE)
 
         spax_scales = gather(spax_scales_raw[:], spax_list, U8, "spax_scales")
         spax_codes = [gather(spax_words[a][:], spax_list, U32, "spax_codes%d" % a) for a in range(2)]
-        w1_mx = [quantize(round_plain(w1_raw[a])[:], "w1_%d" % a) for a in range(2)]
-        sky_place(rest, held([P, S], F32, "h2_last", "w1_raw1"), wg2_gained[2], sky_pages[1], WHOLE)
+        w1_mx = [quantize_held(round_plain(w1_raw[a]), "w1_%d" % a) for a in range(2)]
+        sky_place(rest, held([P, S], F32, "h2_slot2", "w1_raw1"), wg2_gained[2], sky_pages[1], WHOLE)
 
         wd_raw = load_rows(wd, "wd_raw", "w1_raw0")
         wo_raw = held([P, 2, N], I32, "wo_raw")
         nc.sync.dma_start(wo_raw[:], wo_words.rearrange("a p c i -> p a (c i)").bitcast(I32))
-        load_scales_stacked(nc.sync, wo_scales_raw, wo_scales)
+        load_scales_stacked(wo_scales_raw, wo_scales)
 
         def spax_place(s):
-            x = bank(s % 2, [P, S])
+            pre = bank(s % 2, [P, S])
             for a in range(2):
                 nc.tensor.matmul_mx(
-                    out=x[:],
+                    out=pre[:],
                     lhsT=w1_mx[a][0][:, P * s : P * (s + 1)].bitcast(FP8X4),
                     lhsT_scale=w1_mx[a][1][:, P * s : P * (s + 1)],
                     rhs=spax_codes[a][:].bitcast(FP8X4),
@@ -270,14 +284,14 @@ def tile_list_spaxel_sky_kinematics_kernel(
                     start=(a == 0),
                     stop=(a == 1),
                 )
-            h1 = staged([P, S], F32, "h", 3)
-            nc.scalar.activation(h1[:], x[:], ACT.Tanh)
+            h1 = staged([P, S], F32, "h", H_BUFS)
+            nc.scalar.activation(h1[:], pre[:], ACT.Tanh)
             weights = gained(wg1_rows, s, "wg1_gained%d" % s)
             page = spax_pages[s % 2]
             nc.vector.tensor_tensor(page[:].indirect(spax_places[:]), h1[:], weights[:], ALU.mult)
             return page
 
-        z_turned = [held([P, BANK_CHUNKS, H], BF16, "z_turned%d" % h) for h in range(2)]
+        z_turned = [held([P, BANK_CHUNKS, 2, H // 2], BF16, "z_turned%d" % h) for h in range(2)]
 
         def gained_template(s):
             if s != LAST:
@@ -286,16 +300,20 @@ def tile_list_spaxel_sky_kinematics_kernel(
 
         def round_turned(s):
             for h in range(2):
-                nc.scalar.copy(z_turned[h][:, :, P * s : P * (s + 1)], sums[s][h][:])
+                nc.scalar.copy(
+                    z_turned[h][:, :, :, 2 * PAIRS * s : 2 * PAIRS * (s + 1)].rearrange("j c u (p e) -> j c u p e", e=2),
+                    z_sums[s][h][:].rearrange("j c (p u e) -> j c u p e", u=2, e=2),
+                )
 
         def round_last_turned(first, count):
             h, c = divmod(first, BANK_CHUNKS)
-            nc.vector.tensor_tensor(
-                z_turned[h][:, c : c + count, P * LAST :],
-                sums[LAST][h][:, c : c + count, :],
-                gz_last[:].unsqueeze(1).to_broadcast([P, count, P]),
-                ALU.mult,
-            )
+            for u in range(2):
+                nc.vector.tensor_tensor(
+                    z_turned[h][:, c : c + count, u, 2 * PAIRS * LAST :].rearrange("j c (p e) -> j c p e", e=2),
+                    z_sums[LAST][h][:, c : c + count, :].rearrange("j c (p u e) -> j c u p e", u=2, e=2)[:, :, u],
+                    gz_last[:, u, :].rearrange("j (p e) -> j p e", e=2).unsqueeze(1).to_broadcast([P, count, PAIRS, 2]),
+                    ALU.mult,
+                )
 
         for s in range(2):
             add_turned(s, spax_place(s))
@@ -313,46 +331,48 @@ def tile_list_spaxel_sky_kinematics_kernel(
         wd_rounded = round_dealt(wd_raw)
         add_turned(LAST, placed, last=True)
 
-        wq_codes = held([P, 2, 512], U32, "wq_codes", "wg1_rows")
-        wq_scales = held([P, 2, 512], U8, "wq_scales")
-        wq_mx = [(wq_codes[:, a, :], wq_scales[:, a, :]) for a in range(2)]
+        wq_codes = held([P, 2, PASS], U32, "wq_codes", "wg1_rows")
+        wq_scales = held([P, 2, PASS], U8, "wq_scales")
 
         def z_group(g, c0, count):
-            back = bank(6 + g % 2, [P, 2, count * CHUNK])
+            back = bank(BACK_BANK + g % 2, [P, 2, count * CHUNK])
             for c in range(count):
-                words = z_turned[(c0 + c) // BANK_CHUNKS][:, (c0 + c) % BANK_CHUNKS, :].bitcast(F32)
                 for u in range(2):
-                    nc.tensor.transpose(back[:, u, CHUNK * c : CHUNK * (c + 1)], words[:, u : H // 2 : 2], identity[:])
+                    words = z_turned[(c0 + c) // BANK_CHUNKS][:, (c0 + c) % BANK_CHUNKS, u, :].bitcast(F32)
+                    nc.tensor.transpose(back[:, u, CHUNK * c : CHUNK * (c + 1)], words, identity[:])
             if g == 0:
                 z_rounded = held([P, PACK * count * CHUNK], BF16, "z_first", "w1_raw0")
             else:
-                z_rounded = staged([P, PACK * count * CHUNK], BF16, "z_rounded", 2)
+                z_rounded = staged([P, PACK * count * CHUNK], BF16, "z_rounded")
             nc.scalar.copy(
                 z_rounded[:].bitcast(F32).rearrange("p (j u) -> p j u", u=2), back[:].rearrange("p u j -> p j u")
             )
-            codes, scales = quantize(z_rounded[:], "z_%d" % g)
+            codes, scales = quantize_held(z_rounded[:], "z_%d" % g)
             return [(codes[:, CHUNK * c : CHUNK * (c + 1)], scales[:, CHUNK * c : CHUNK * (c + 1)]) for c in range(count)]
 
         def f_sums(c, z_chunk):
-            bent = staged([P, 2, CHUNK, PACK], F32, "bent", 5)
+            bent = staged([P, 2, CHUNK, PACK], F32, "bent", BENT_BUFS)
             for a in range(2):
-                sums = bank(4 - 2 * (c % 2) + a, [P, PACK, CHUNK])
+                pre = bank(F_BANKS[c % 2] + a, [P, PACK, CHUNK])
                 for t in range(PACK):
                     nc.tensor.matmul_mx(
-                        out=sums[:, t, :],
-                        lhsT=wq_mx[a][0][:, P * t : P * (t + 1)].bitcast(FP8X4),
-                        lhsT_scale=wq_mx[a][1][:, P * t : P * (t + 1)],
+                        out=pre[:, t, :],
+                        lhsT=wq_codes[:, a, P * t : P * (t + 1)].bitcast(FP8X4),
+                        lhsT_scale=wq_scales[:, a, P * t : P * (t + 1)],
                         rhs=z_chunk[0].bitcast(FP8X4),
                         rhs_scale=z_chunk[1],
                         start=True,
                         stop=True,
                     )
-                nc.scalar.activation(bent[:, a], sums[:].rearrange("p t j -> p j t"), ACT.Tanh)
+                nc.scalar.activation(bent[:, a], pre[:].rearrange("p t j -> p j t"), ACT.Tanh)
             return bent
 
+        def f_parts(c):
+            return PASS_BY_PASS if c in (0, CHUNKS - 1) else BOTH_PASSES
+
         def f_round(c, bent):
-            f_rounded = staged([P, 2, CHUNK, PACK], BF16, "f_rounded", 2)
-            for part in F_PARTS[c in (0, CHUNKS - 1)]:
+            f_rounded = staged([P, 2, CHUNK, PACK], BF16, "f_rounded")
+            for part in f_parts(c):
                 shape = [P, part.stop - part.start, CHUNK, PACK]
                 nc.vector.tensor_tensor(
                     f_rounded[:, part], bent[:, part], gf_cols[:, part].unsqueeze(2).to_broadcast(shape), ALU.mult
@@ -361,9 +381,12 @@ def tile_list_spaxel_sky_kinematics_kernel(
 
         def f_quantize(c, f_rounded):
             operands = []
-            for part in F_PARTS[c in (0, CHUNKS - 1)]:
-                codes, scales = quantize(f_rounded[:, part].rearrange("p a j t -> p (a j t)"), "f", 3)
-                for a in range(part.stop - part.start):
+            for part in f_parts(c):
+                passes = part.stop - part.start
+                codes = staged([P, passes * CHUNK], U32, "f_codes", F_BUFS)
+                scales = staged([P, passes * CHUNK], U8, "f_scales", F_BUFS)
+                quantize(f_rounded[:, part].rearrange("p a j t -> p (a j t)"), codes[:], scales[:])
+                for a in range(passes):
                     cols = slice(CHUNK * a, CHUNK * (a + 1))
                     operands.append((codes[:, cols], scales[:, cols]))
             return operands
@@ -376,28 +399,23 @@ def tile_list_spaxel_sky_kinematics_kernel(
         codes_out = out_1[0].rearrange("p j t -> p (j t)").bitcast(I32)
 
         def y_sums(c, f_mx, z_chunk):
-            sums = bank(c % 2, [P, PACK, CHUNK])
-            passes = [(wd_mx[0][:], wd_mx[1][:], z_chunk)]
-            passes.extend((wo_codes[:, a, :], wo_scale_planes[4 * a :, :], f_mx[a]) for a in range(2))
-            for n, (codes, scales, moving) in enumerate(passes):
+            total = bank(c % 2, [P, PACK, CHUNK])
+            products = [(wd_mx[0], wd_mx[1], z_chunk)]
+            products.extend((wo_codes[:, a, :], wo_scale_planes[4 * a :, :], f_mx[a]) for a in range(2))
+            for n, (codes, scales, moving) in enumerate(products):
                 for t in range(PACK):
                     cols = slice(P * t, P * (t + 1))
                     nc.tensor.matmul_mx(
-                        out=sums[:, t, :],
+                        out=total[:, t, :],
                         lhsT=codes[:, cols].bitcast(FP8X4),
                         lhsT_scale=scales[:, cols],
                         rhs=moving[0].bitcast(FP8X4),
                         rhs_scale=moving[1],
                         start=(n == 0 and t == 0),
-                        stop=(n == len(passes) - 1 and t == PACK - 1),
+                        stop=(n == len(products) - 1 and t == PACK - 1),
                     )
             j0 = CHUNK * (c % BANK_CHUNKS)
-            rows = y_rows[c // BANK_CHUNKS][:, :, j0 : j0 + CHUNK]
-            nc.scalar.copy(rows, sums[:])
-            if c in Y_ON_SCALAR:
-                nc.scalar.copy(
-                    y_rounded[c // BANK_CHUNKS][:, j0 : j0 + CHUNK, :], sums[:].rearrange("p t j -> p j t")
-                )
+            nc.scalar.copy(y_rows[c // BANK_CHUNKS][:, :, j0 : j0 + CHUNK], total[:])
             if c % 2 == 1 or c == CHUNKS - 2:
                 first = c - 1 if c < CHUNKS - 2 else c
                 nc.sync.dma_start(
@@ -406,33 +424,35 @@ def tile_list_spaxel_sky_kinematics_kernel(
                 )
 
         def y_planes(first, count):
-            half = first // BANK_CHUNKS
+            h = first // BANK_CHUNKS
             for c in range(first, first + count):
-                if c not in Y_ON_SCALAR:
-                    cols = slice(CHUNK * (c % BANK_CHUNKS), CHUNK * (c % BANK_CHUNKS + 1))
-                    nc.vector.tensor_copy(
-                        y_rounded[half][:, cols, :].rearrange("p (c n) t -> p c t n", n=4),
-                        y_rows[half][:, :, cols].rearrange("p t (c n) -> p c t n", n=4),
-                    )
+                cols = slice(CHUNK * (c % BANK_CHUNKS), CHUNK * (c % BANK_CHUNKS + 1))
+                nc.vector.tensor_copy(
+                    y_rounded[h][:, cols, :].rearrange("p (c n) t -> p c t n", n=LINE),
+                    y_rows[h][:, :, cols].rearrange("p t (c n) -> p c t n", n=LINE),
+                )
             j0 = CHUNK * (first % BANK_CHUNKS)
             cols = slice(CHUNK * first, CHUNK * (first + count))
-            nc.vector.quantize_mx(
-                out=y_codes[:, cols].bitcast(FP8X4),
-                scales=y_scales[:, cols],
-                in_=y_rounded[half][:, j0 : j0 + CHUNK * count, :].rearrange("p j t -> p (j t)"),
+            quantize(
+                y_rounded[h][:, j0 : j0 + CHUNK * count, :].rearrange("p j t -> p (j t)"),
+                y_codes[:, cols],
+                y_scales[:, cols],
             )
             nc.sync.dma_start(codes_out[:, cols], y_codes[:, cols].bitcast(I32))
 
         z_chunks = []
+        bents, f_roundeds, f_mxs = {}, {}, {}
         for g, count in enumerate(Z_GROUPS):
             if g < len(LAST_ROUNDS):
                 round_last_turned(*LAST_ROUNDS[g])
             z_chunks.extend(z_group(g, len(z_chunks), count))
             if g == 0:
                 for a in range(2):
-                    nc.vector.quantize_mx(out=wq_mx[a][0].bitcast(FP8X4), scales=wq_mx[a][1], in_=wq_rounded[a][:])
-            if g == 2:
-                wd_mx = quantize(wd_rounded[:], "wd")
+                    quantize(wq_rounded[a], wq_codes[:, a, :], wq_scales[:, a, :])
+            if g < EARLY_F:
+                bents[g] = f_sums(g, z_chunks[g])
+            if g == EARLY_F:
+                wd_mx = quantize_held(wd_rounded, "wd")
                 wo_codes = held([P, 2, N], U32, "wo_codes")
                 nc.vector.tensor_copy(
                     wo_codes[:].bitcast(I32).rearrange("p a (t q) -> p a q t", t=PACK),
@@ -444,7 +464,6 @@ def tile_list_spaxel_sky_kinematics_kernel(
                     wo_scales_raw[:].rearrange("p (q t) -> p t q", t=PACK),
                 )
 
-        bents, f_roundeds, f_mxs = {}, {}, {}
         for step in range(CHUNKS + 3):
             c = step - 3
             if 0 <= c < CHUNKS:
@@ -456,11 +475,12 @@ def tile_list_spaxel_sky_kinematics_kernel(
             if 0 <= c < CHUNKS:
                 f_roundeds[c] = f_round(c, bents[c])
             c = step
-            if c < CHUNKS:
+            if EARLY_F <= c < CHUNKS:
                 bents[c] = f_sums(c, z_chunks[c])
 
-        for first, count in ((0, 4), (4, 3), (7, 1)):
+        for first, count in PLANE_CALLS:
             y_planes(first, count)
-
         for q in range(QUADS):
-            nc.sync.dma_start(out_2[0, 4 * q : 4 * q + 4, :].bitcast(I32), y_scales[32 * q : 32 * q + 4, :].bitcast(I32))
+            nc.sync.dma_start(
+                out_2[0, 4 * q : 4 * q + 4, :].bitcast(I32), y_scales[32 * q : 32 * q + 4, :].bitcast(I32)
+            )

import math
from contextlib import ExitStack

import concourse.mybir as mybir
from concourse.masks import make_identity

K, T, S, T2, H, M, N = 1024, 2048, 512, 1024, 512, 1024, 512
FLOPS = 2 * (2 * K * H * S + H * M * T2 + M * N * T2 + H * N * T2)

F32 = mybir.dt.float32
BF16 = mybir.dt.bfloat16
I32 = mybir.dt.int32
U32 = mybir.dt.uint32
U16 = mybir.dt.uint16
U8 = mybir.dt.uint8
FP8X4 = mybir.dt.float8_e4m3fn_x4
FP4X4 = mybir.dt.float4_e2m1fn_x4
ALU = mybir.AluOpType
ACT = mybir.ActivationFunctionType

P = 128
PACK = 4
PASS = P * PACK
QUADS = 4
STRIPE = 16
LINE = 4
SLOTS = H // P
LAST = SLOTS - 1
CHUNK = 128
CHUNKS = T2 // CHUNK
BANK_CHUNKS = 4
PAIRS = P // PACK

SUM_BANKS = (4, 6, 4, 2)
BACK_BANK = 6
F_BANKS = (4, 2)

HALVES = (slice(0, S // 2), slice(S // 2, S))
WHOLE = slice(0, S)
LAST_ROUNDS = ((0, 1), (1, BANK_CHUNKS - 1), (BANK_CHUNKS, BANK_CHUNKS))
Z_GROUPS = (1, 1, 2, 2, 2)
EARLY_F = 2
BOTH_PASSES = (slice(0, 2),)
PASS_BY_PASS = (slice(0, 1), slice(1, 2))
PLANE_CALLS = ((0, BANK_CHUNKS), (BANK_CHUNKS, BANK_CHUNKS - 1), (CHUNKS - 1, 1))
ROUNDED_BUFS, BENT_BUFS, H_BUFS, F_BUFS = 3, 5, 3, 3
ROUND = 1.5 * 2.0**23


def tile_list_spaxel_sky_kinematics_kernel(
    tc, tab_words, tab_scales, tab2_words, tab2_scales, offs, offs2, offs3, offs4, w1, w2_words, w2_scales,
    wg1, wg2, tpl, gz, wq, gf, wo_words, wo_scales, wd, out_0, out_1, out_2,
):
    nc = tc.nc
    with ExitStack() as ctx:
        lists = ctx.enter_context(tc.tile_pool(name="lists", bufs=1))
        keep = ctx.enter_context(tc.tile_pool(name="keep", bufs=1))
        ring = ctx.enter_context(tc.tile_pool(name="ring", bufs=2))
        psum = ctx.enter_context(tc.psum_pool(name="psum", bufs=1))

        def held(shape, dtype, name, after=None):
            return keep.tile(shape, dtype, name=name, tag=after or name, align_bytes=64)

        def staged(shape, dtype, name, bufs=2):
            return ring.tile(shape, dtype, name=name, tag=name, bufs=bufs, align_bytes=64)

        def bank(number, shape):
            return psum.tile(shape, F32, name="bank%d" % number, tag="bank%d" % number)

        def load_list(source, name):
            tile = lists.tile([P, S // STRIPE], U16, name=name)
            nc.sync.dma_start(tile[:], source)
            return tile

        def load_words(words, a, name):
            tile = held([P, T], U32, name)
            nc.sync.dma_start(tile[:].bitcast(I32), words[a].rearrange("p t i -> p (t i)").bitcast(I32))
            return tile

        def load_scales_side_by_side(tile, scales):
            for q in range(QUADS):
                nc.sync.dma_start(
                    tile[32 * q : 32 * q + 4, :].bitcast(I32).rearrange("r (a w) -> r a w", a=2),
                    scales[:, 4 * q : 4 * q + 4, :].rearrange("a r c -> r a c").bitcast(I32),
                )

        def load_scales_stacked(tile, scales):
            for q in range(QUADS):
                nc.sync.dma_start(
                    tile[32 * q : 32 * q + 8, :].bitcast(I32), scales[:, 4 * q : 4 * q + 4, :].bitcast(I32)
                )

        def load_rows(rows, name, after=None):
            tile = held([P, PACK, rows.shape[1]], F32, name, after)
            nc.sync.dma_start(tile[:], rows.rearrange("(p i) c -> p i c", i=PACK))
            return tile

        def entries(offsets, part):
            return offsets[:, part.start // STRIPE : part.stop // STRIPE]

        def gather(window, offsets, dtype, name):
            picked = held([P, S], dtype, name)
            nc.vector.tensor_copy(picked[:], window.indirect(offsets[:]))
            return picked

        def quantize(rounded, codes, scales):
            nc.vector.quantize_mx(out=codes.bitcast(FP8X4), scales=scales, in_=rounded)
            return codes, scales

        def quantize_held(rounded, name):
            width = rounded.shape[1] // PACK
            codes = held([P, width], U32, name + "_codes")
            scales = held([P, width], U8, name + "_scales")
            return quantize(rounded, codes[:], scales[:])

        def round_plain(raw):
            rounded = staged([P, PASS, PACK], BF16, "rounded", ROUNDED_BUFS)
            for half in range(2):
                cols = slice(PASS // 2 * half, PASS // 2 * (half + 1))
                nc.scalar.copy(
                    rounded[:, cols, :].rearrange("p (c n) i -> p c i n", n=LINE),
                    raw[:, :, cols].rearrange("p i (c n) -> p c i n", n=LINE),
                )
            return rounded[:].rearrange("p c i -> p (c i)")

        def round_dealt(raw):
            rounded = staged([P, PASS, PACK], BF16, "rounded", ROUNDED_BUFS)
            dealt = rounded[:].rearrange("p (t q) i -> p q i t", t=PACK)
            source = raw[:].rearrange("p i (q t) -> p q i t", t=PACK)
            for half in range(2):
                nc.scalar.copy(dealt[:, :, :, 2 * half : 2 * half + 2], source[:, :, :, 2 * half : 2 * half + 2])
            return rounded[:].rearrange("p c i -> p (c i)")

        sky_scales_raw = held([P, 2 * T], U8, "sky_scales_raw")
        nc.vector.memset(sky_scales_raw[:].bitcast(I32), 0)
        w2_scale_planes = held([P, 2 * H], U8, "w2_scale_planes")
        nc.gpsimd.memset(w2_scale_planes[:].bitcast(I32), 0)
        spax_scales_raw = held([P, T], U8, "spax_scales_raw")
        nc.gpsimd.memset(spax_scales_raw[:].bitcast(I32), 0)
        wo_scales_raw = held([P, N], U8, "wo_scales_raw")
        nc.gpsimd.memset(wo_scales_raw[:].bitcast(I32), 0)
        warm = held([P, 1], F32, "warm")
        nc.vector.memset(warm[:], 0.0)
        nc.scalar.activation(warm[:], warm[:], ACT.Silu)

        sky_list = load_list(offs2, "sky_list")
        sky_places = load_list(offs4, "sky_places")
        spax_list = load_list(offs, "spax_list")
        spax_places = load_list(offs3, "spax_places")
        gf_cols = held([P, 2, PACK], F32, "gf_cols")
        nc.sync.dma_start(gf_cols[:], gf.rearrange("(a p t) -> p a t", a=2, t=PACK))
        sky_words = [load_words(tab2_words, 0, "sky_words0")]
        gz_cols = held([P, SLOTS], F32, "gz_cols")
        with nc.allow_non_contiguous_dma(reason="one gain a partition and slot"):
            nc.sync.dma_start(gz_cols[:], gz.rearrange("(s p) -> p s", p=P))
        wg2_rows = held([P, S], F32, "wg2_rows")
        nc.sync.dma_start(wg2_rows[:], wg2)
        load_scales_side_by_side(sky_scales_raw, tab2_scales)
        sky_words.append(load_words(tab2_words, 1, "sky_words1"))
        w2_codes = held([P, 2, 2 * H], U8, "w2_codes")
        nc.sync.dma_start(w2_codes[:].bitcast(I32), w2_words.rearrange("a p c -> p a c").bitcast(I32))
        load_scales_side_by_side(w2_scale_planes, w2_scales)
        spax_words = [load_words(tab_words, 0, "spax_words0")]
        load_scales_stacked(spax_scales_raw, tab_scales)
        spax_words.append(load_words(tab_words, 1, "spax_words1"))
        wg1_rows = held([P, S], F32, "wg1_rows")
        nc.sync.dma_start(wg1_rows[:], wg1)
        w1_raw = [load_rows(w1[PASS * a : PASS * (a + 1), :], "w1_raw%d" % a) for a in range(2)]

        identity = held([P, P], F32, "identity")
        make_identity(nc, identity[:])

        sky_codes = [gather(sky_words[0][:], sky_list, U32, "sky_codes0")]
        sky_scales = [
            gather(sky_scales_raw[:, a * T : (a + 1) * T], sky_list, U8, "sky_scales%d" % a) for a in range(2)
        ]
        sky_codes.append(held([P, S], U32, "sky_codes1"))
        for part in HALVES:
            nc.vector.tensor_copy(sky_codes[1][:, part], sky_words[1][:].indirect(entries(sky_list, part)))

        wq_raw = [load_rows(wq[:, PASS * a : PASS * (a + 1)], "wq_raw%d" % a, "sky_words%d" % a) for a in range(2)]
        tpl_rows = []
        for s in range(SLOTS):
            rows = held([P, T2], F32, "tpl_rows%d" % s)
            nc.sync.dma_start(rows[:], tpl[P * s : P * (s + 1), :])
            tpl_rows.append(rows)

        sky_pages = [held([P, T2], F32, "sky_page%d" % n) for n in range(2)]
        spax_pages = [held([P, T2], F32, "spax_page%d" % n) for n in range(2)]
        for page in sky_pages + spax_pages:
            nc.vector.memset(page[:], 0.0)

        gz_spread = bank(0, [P, P])
        nc.tensor.transpose(gz_spread[:], gz_cols[:, LAST : LAST + 1].to_broadcast([P, P]), identity[:])
        gz_last = held([P, 2, 2 * PAIRS], F32, "gz_last")
        nc.scalar.copy(
            gz_last[:].rearrange("j u (p e) -> j u p e", e=2),
            gz_spread[:].rearrange("j (p u e) -> j u p e", u=2, e=2),
        )

        z_sums = {}

        def add_turned(s, term, first=False, last=False):
            if first:
                z_sums[s] = [bank(SUM_BANKS[s] + h, [P, BANK_CHUNKS, P]) for h in range(2)]
            for h in range(2):
                for c in range(BANK_CHUNKS):
                    j0 = CHUNK * (BANK_CHUNKS * h + c)
                    nc.tensor.matmul(
                        z_sums[s][h][:, c, :],
                        term[:, j0 : j0 + CHUNK],
                        identity[:],
                        is_transpose=True,
                        start=(first and c == 0),
                        stop=(last and c == BANK_CHUNKS - 1),
                    )

        def gained(rows, s, name):
            if s == LAST:
                return rows
            scaled = held([P, S], F32, name)
            nc.scalar.activation(scaled[:], rows[:], ACT.Copy, scale=gz_cols[:, s : s + 1])
            return scaled

        def sky_rest(s, number, part):
            width = part.stop - part.start
            angle = bank(number, [P, width])
            for a in range(2):
                nc.tensor.matmul_mx(
                    out=angle[:],
                    lhsT=w2_codes[:, a, 2 * P * s : 2 * P * (s + 1)].bitcast(FP4X4),
                    lhsT_scale=w2_scale_planes[:, a * H + P * s : a * H + P * (s + 1)],
                    rhs=sky_codes[a][:, part].bitcast(FP8X4),
                    rhs_scale=sky_scales[a][:, part],
                    start=(a == 0),
                    stop=(a == 1),
                )
            turns = staged([P, width], F32, "turns")
            nc.scalar.activation(turns[:], angle[:], ACT.Copy, scale=1.0 / (2.0 * math.pi))
            whole = staged([P, width], U32, "whole")
            nc.scalar.activation(whole[:], turns[:], ACT.Copy, bias=ROUND)
            rest = staged([P, width], F32, "rest")
            nc.vector.scalar_tensor_tensor(
                rest[:], whole[:].bitcast(I32), ROUND, turns[:], ALU.subtract, ALU.subtract
            )
            return rest

        def sky_place(rest, h2, weights, page, part):
            nc.scalar.activation(h2[:], rest[:], ACT.Sin, scale=-2.0 * math.pi)
            nc.vector.tensor_tensor(
                page[:].indirect(entries(sky_places, part)), h2[:], weights[:, part], ALU.mult
            )

        wg2_gained = [gained(wg2_rows, s, "wg2_gained%d" % s) for s in range(SLOTS)]
        for n, part in enumerate(HALVES):
            rest = sky_rest(LAST, n, part)
            sky_place(rest, staged([P, S // 2], F32, "h", H_BUFS), wg2_gained[LAST], sky_pages[0], part)
        add_turned(LAST, sky_pages[0], first=True)
        for s in range(2):
            rest = sky_rest(s, s, WHOLE)
            sky_place(rest, staged([P, S], F32, "h", H_BUFS), wg2_gained[s], sky_pages[1 - s], WHOLE)
            add_turned(s, sky_pages[1 - s], first=True)
        rest = sky_rest(2, 0, WHOLE)

        spax_scales = gather(spax_scales_raw[:], spax_list, U8, "spax_scales")
        spax_codes = [gather(spax_words[a][:], spax_list, U32, "spax_codes%d" % a) for a in range(2)]
        w1_mx = [quantize_held(round_plain(w1_raw[a]), "w1_%d" % a) for a in range(2)]
        sky_place(rest, held([P, S], F32, "h2_slot2", "w1_raw1"), wg2_gained[2], sky_pages[1], WHOLE)

        wd_raw = load_rows(wd, "wd_raw", "w1_raw0")
        wo_raw = held([P, 2, N], I32, "wo_raw")
        nc.sync.dma_start(wo_raw[:], wo_words.rearrange("a p c i -> p a (c i)").bitcast(I32))
        load_scales_stacked(wo_scales_raw, wo_scales)

        def spax_place(s):
            pre = bank(s % 2, [P, S])
            for a in range(2):
                nc.tensor.matmul_mx(
                    out=pre[:],
                    lhsT=w1_mx[a][0][:, P * s : P * (s + 1)].bitcast(FP8X4),
                    lhsT_scale=w1_mx[a][1][:, P * s : P * (s + 1)],
                    rhs=spax_codes[a][:].bitcast(FP8X4),
                    rhs_scale=spax_scales[4 * a :, :],
                    start=(a == 0),
                    stop=(a == 1),
                )
            h1 = staged([P, S], F32, "h", H_BUFS)
            nc.scalar.activation(h1[:], pre[:], ACT.Tanh)
            weights = gained(wg1_rows, s, "wg1_gained%d" % s)
            page = spax_pages[s % 2]
            nc.vector.tensor_tensor(page[:].indirect(spax_places[:]), h1[:], weights[:], ALU.mult)
            return page

        z_turned = [held([P, BANK_CHUNKS, 2, H // 2], BF16, "z_turned%d" % h) for h in range(2)]

        def gained_template(s):
            if s != LAST:
                nc.scalar.activation(tpl_rows[s][:], tpl_rows[s][:], ACT.Copy, scale=gz_cols[:, s : s + 1])
            return tpl_rows[s]

        def round_turned(s):
            for h in range(2):
                nc.scalar.copy(
                    z_turned[h][:, :, :, 2 * PAIRS * s : 2 * PAIRS * (s + 1)].rearrange("j c u (p e) -> j c u p e", e=2),
                    z_sums[s][h][:].rearrange("j c (p u e) -> j c u p e", u=2, e=2),
                )

        def round_last_turned(first, count):
            h, c = divmod(first, BANK_CHUNKS)
            for u in range(2):
                nc.vector.tensor_tensor(
                    z_turned[h][:, c : c + count, u, 2 * PAIRS * LAST :].rearrange("j c (p e) -> j c p e", e=2),
                    z_sums[LAST][h][:, c : c + count, :].rearrange("j c (p u e) -> j c u p e", u=2, e=2)[:, :, u],
                    gz_last[:, u, :].rearrange("j (p e) -> j p e", e=2).unsqueeze(1).to_broadcast([P, count, PAIRS, 2]),
                    ALU.mult,
                )

        for s in range(2):
            add_turned(s, spax_place(s))
        wq_rounded = [round_dealt(wq_raw[a]) for a in range(2)]
        placed = spax_place(2)
        for s in range(2):
            add_turned(s, gained_template(s), last=True)
            round_turned(s)
        add_turned(2, sky_pages[1], first=True)
        add_turned(2, gained_template(2))
        add_turned(LAST, gained_template(LAST))
        add_turned(2, placed, last=True)
        placed = spax_place(LAST)
        round_turned(2)
        wd_rounded = round_dealt(wd_raw)
        add_turned(LAST, placed, last=True)

        wq_codes = held([P, 2, PASS], U32, "wq_codes", "wg1_rows")
        wq_scales = held([P, 2, PASS], U8, "wq_scales")

        def z_group(g, c0, count):
            back = bank(BACK_BANK + g % 2, [P, 2, count * CHUNK])
            for c in range(count):
                for u in range(2):
                    words = z_turned[(c0 + c) // BANK_CHUNKS][:, (c0 + c) % BANK_CHUNKS, u, :].bitcast(F32)
                    nc.tensor.transpose(back[:, u, CHUNK * c : CHUNK * (c + 1)], words, identity[:])
            if g == 0:
                z_rounded = held([P, PACK * count * CHUNK], BF16, "z_first", "w1_raw0")
            else:
                z_rounded = staged([P, PACK * count * CHUNK], BF16, "z_rounded")
            nc.scalar.copy(
                z_rounded[:].bitcast(F32).rearrange("p (j u) -> p j u", u=2), back[:].rearrange("p u j -> p j u")
            )
            codes, scales = quantize_held(z_rounded[:], "z_%d" % g)
            return [(codes[:, CHUNK * c : CHUNK * (c + 1)], scales[:, CHUNK * c : CHUNK * (c + 1)]) for c in range(count)]

        def f_sums(c, z_chunk):
            bent = staged([P, 2, CHUNK, PACK], F32, "bent", BENT_BUFS)
            for a in range(2):
                pre = bank(F_BANKS[c % 2] + a, [P, PACK, CHUNK])
                for t in range(PACK):
                    nc.tensor.matmul_mx(
                        out=pre[:, t, :],
                        lhsT=wq_codes[:, a, P * t : P * (t + 1)].bitcast(FP8X4),
                        lhsT_scale=wq_scales[:, a, P * t : P * (t + 1)],
                        rhs=z_chunk[0].bitcast(FP8X4),
                        rhs_scale=z_chunk[1],
                        start=True,
                        stop=True,
                    )
                nc.scalar.activation(bent[:, a], pre[:].rearrange("p t j -> p j t"), ACT.Tanh)
            return bent

        def f_parts(c):
            return PASS_BY_PASS if c in (0, CHUNKS - 1) else BOTH_PASSES

        def f_round(c, bent):
            f_rounded = staged([P, 2, CHUNK, PACK], BF16, "f_rounded")
            for part in f_parts(c):
                shape = [P, part.stop - part.start, CHUNK, PACK]
                nc.vector.tensor_tensor(
                    f_rounded[:, part], bent[:, part], gf_cols[:, part].unsqueeze(2).to_broadcast(shape), ALU.mult
                )
            return f_rounded

        def f_quantize(c, f_rounded):
            operands = []
            for part in f_parts(c):
                passes = part.stop - part.start
                codes = staged([P, passes * CHUNK], U32, "f_codes", F_BUFS)
                scales = staged([P, passes * CHUNK], U8, "f_scales", F_BUFS)
                quantize(f_rounded[:, part].rearrange("p a j t -> p (a j t)"), codes[:], scales[:])
                for a in range(passes):
                    cols = slice(CHUNK * a, CHUNK * (a + 1))
                    operands.append((codes[:, cols], scales[:, cols]))
            return operands

        y_rows = [held([P, PACK, T2 // 2], F32, "y_rows%d" % h, "spax_words%d" % h) for h in range(2)]
        y_rounded = [held([P, T2 // 2, PACK], BF16, "y_rounded%d" % h) for h in range(2)]
        y_codes = held([P, T2], U32, "y_codes")
        y_scales = held([P, T2], U8, "y_scales")
        y_out = out_0.rearrange("(p t) j -> p t j", t=PACK)
        codes_out = out_1[0].rearrange("p j t -> p (j t)").bitcast(I32)

        def y_sums(c, f_mx, z_chunk):
            total = bank(c % 2, [P, PACK, CHUNK])
            products = [(wd_mx[0], wd_mx[1], z_chunk)]
            products.extend((wo_codes[:, a, :], wo_scale_planes[4 * a :, :], f_mx[a]) for a in range(2))
            for n, (codes, scales, moving) in enumerate(products):
                for t in range(PACK):
                    cols = slice(P * t, P * (t + 1))
                    nc.tensor.matmul_mx(
                        out=total[:, t, :],
                        lhsT=codes[:, cols].bitcast(FP8X4),
                        lhsT_scale=scales[:, cols],
                        rhs=moving[0].bitcast(FP8X4),
                        rhs_scale=moving[1],
                        start=(n == 0 and t == 0),
                        stop=(n == len(products) - 1 and t == PACK - 1),
                    )
            j0 = CHUNK * (c % BANK_CHUNKS)
            nc.scalar.copy(y_rows[c // BANK_CHUNKS][:, :, j0 : j0 + CHUNK], total[:])
            if c % 2 == 1 or c == CHUNKS - 2:
                first = c - 1 if c < CHUNKS - 2 else c
                nc.sync.dma_start(
                    y_out[:, :, CHUNK * first : CHUNK * (c + 1)],
                    y_rows[c // BANK_CHUNKS][:, :, CHUNK * (first % BANK_CHUNKS) : j0 + CHUNK],
                )

        def y_planes(first, count):
            h = first // BANK_CHUNKS
            for c in range(first, first + count):
                cols = slice(CHUNK * (c % BANK_CHUNKS), CHUNK * (c % BANK_CHUNKS + 1))
                nc.vector.tensor_copy(
                    y_rounded[h][:, cols, :].rearrange("p (c n) t -> p c t n", n=LINE),
                    y_rows[h][:, :, cols].rearrange("p t (c n) -> p c t n", n=LINE),
                )
            j0 = CHUNK * (first % BANK_CHUNKS)
            cols = slice(CHUNK * first, CHUNK * (first + count))
            quantize(
                y_rounded[h][:, j0 : j0 + CHUNK * count, :].rearrange("p j t -> p (j t)"),
                y_codes[:, cols],
                y_scales[:, cols],
            )
            nc.sync.dma_start(codes_out[:, cols], y_codes[:, cols].bitcast(I32))

        z_chunks = []
        bents, f_roundeds, f_mxs = {}, {}, {}
        for g, count in enumerate(Z_GROUPS):
            if g < len(LAST_ROUNDS):
                round_last_turned(*LAST_ROUNDS[g])
            z_chunks.extend(z_group(g, len(z_chunks), count))
            if g == 0:
                for a in range(2):
                    quantize(wq_rounded[a], wq_codes[:, a, :], wq_scales[:, a, :])
            if g < EARLY_F:
                bents[g] = f_sums(g, z_chunks[g])
            if g == EARLY_F:
                wd_mx = quantize_held(wd_rounded, "wd")
                wo_codes = held([P, 2, N], U32, "wo_codes")
                nc.vector.tensor_copy(
                    wo_codes[:].bitcast(I32).rearrange("p a (t q) -> p a q t", t=PACK),
                    wo_raw[:].rearrange("p a (q t) -> p a q t", t=PACK),
                )
                wo_scale_planes = held([P, N], U8, "wo_scale_planes")
                nc.vector.tensor_copy(
                    wo_scale_planes[:].rearrange("p (t q) -> p t q", t=PACK),
                    wo_scales_raw[:].rearrange("p (q t) -> p t q", t=PACK),
                )

        for step in range(CHUNKS + 3):
            c = step - 3
            if 0 <= c < CHUNKS:
                y_sums(c, f_mxs[c], z_chunks[c])
            c = step - 2
            if 0 <= c < CHUNKS:
                f_mxs[c] = f_quantize(c, f_roundeds[c])
            c = step - 1
            if 0 <= c < CHUNKS:
                f_roundeds[c] = f_round(c, bents[c])
            c = step
            if EARLY_F <= c < CHUNKS:
                bents[c] = f_sums(c, z_chunks[c])

        for first, count in PLANE_CALLS:
            y_planes(first, count)
        for q in range(QUADS):
            nc.sync.dma_start(
                out_2[0, 4 * q : 4 * q + 4, :].bitcast(I32), y_scales[32 * q : 32 * q + 4, :].bitcast(I32)
            )
